import numpy as np, ml_dtypes
CORES = [13,21,141,149]
N = 4
BF = ml_dtypes.bfloat16
def gentries(a):
    return np.ascontiguousarray(a.reshape(8, 16, -1).transpose(0, 2, 1)).reshape(8, -1)
def gtable(e):
    e = np.asarray(e); return np.ascontiguousarray(e.reshape(8, -1, 16).transpose(0, 2, 1)).reshape(128, -1).astype(np.int32)
S, G, CAP, WN, M, Q, RO, H, T0 = 1792, 384, 32, 160, 512, 2048, 4, 3, 192
W, L = S + (N - 1) * G, (N - 1) * CAP + WN
def lines(rng, n):
    base = rng.integers(0, 256, (N, 8, 1, n)); amp = rng.choice(np.array([0.0, 2.0, 12.0, 50.0]), (N, 8, 1, n))
    return np.clip(np.rint(base + amp * rng.standard_normal((N, 8, 15, n))), 0, 255).astype(np.int64)
def parts(rng):
    st = np.where(rng.random((N, 8, S)) < rng.choice(np.array([0.3, 0.45, 0.6]), (N, 8, 1)), -1, rng.integers(0, T0, (N, 8, S)))
    x = np.concatenate([lines(rng, S), st[:, :, None, :]], axis=2)
    order = np.argsort(st, axis=-1, kind="stable"); pos = np.argsort(order, axis=-1)
    span = rng.choice(np.array([4, 32, 300]), (N, 8, 1, S))
    at = np.clip(pos[:, :, None, :] + (span * (rng.random((N, 8, 16, S)) * 4 - 3)).astype(np.int64), 0, S - 1)
    nb = np.take_along_axis(order[:, :, None, :], at, 3)
    gh = rng.random((N, 8, 16, S)) < rng.choice(np.array([0.01, 0.03, 0.08]), (N, 8, 1, 1))
    nb = np.where(gh, rng.integers(S, W, (N, 8, 16, S)), nb)
    pl = np.concatenate([lines(rng, M), rng.integers(0, 256, (N, 8, 1, M))], axis=2); w = rng.integers(0, 256, (N, 8, 16, 1))
    none = np.sum(st < 0, axis=-1)[:, :, None]; k = np.minimum(none + (rng.random((N, 8, RO * WN)) * (S - none)).astype(np.int64), S - 1)
    wl = np.take_along_axis(order, k, 2); wl = np.where(rng.random(wl.shape) < 0.1, rng.integers(0, S, wl.shape), wl).reshape(N, 8, RO, WN)
    return x, nb, pl, w, wl, rng.integers(0, S, (N, 8, N - 1, G))
def pack(x, nb, pl, w, wl, sl):
    return {"x0": x.reshape(N, 128, S).astype(np.float32).astype(BF), "nb": np.ascontiguousarray(nb.reshape(N, 128, S)).astype(np.int32),
            "pull": pl.reshape(N, 128, M).astype(np.float32).astype(BF), "wt": w.reshape(N, 128, 1).astype(np.int32),
            "wants": np.stack([gtable(a.reshape(8, -1)) for a in wl]), "snd": np.stack([gtable(a.reshape(8, -1)) for a in sl])}
def aim(bl, lo):
    place = np.array([np.sum(bl[:i] == bl[i]) for i in range(len(bl))])
    return S + bl * G + lo + place % CAP
def brim(rng, x, nb, w, wl, sl, g):
    K = (N - 1) * CAP; w[:, g] = 0; w[:, g, 0] = 16; w[:, g, 1] = 1
    for r in range(N):
        zs = rng.permutation(Q); h = ((zs * zs >> 5) + 194) & (Q - 1)
        u, i = np.unique(np.where(h >= S, h - S, h), return_index=True)
        p = rng.permutation(np.nonzero(u)[0])[:L]; z = zs[i[p]]
        o = rng.permutation(np.setdiff1d(np.arange(1, S), u[p]))[:3 * WN + 2 * K]
        o[2 * WN + K + int(rng.integers(0, K))] = 0
        one, two, asked, late, last = np.split(o, [WN, 2 * WN, 2 * WN + K, 2 * WN + 2 * K])
        x[r, g, 15, u[p]] = -1
        for q, k in ((one, 0), (two, 0), (asked, 1), (late, 2)):
            x[r, g, 2, q] = 100 * k + rng.integers(0, 50, len(q)); x[r, g, 3, q] = 250 - 100 * k - rng.integers(0, 50, len(q))
            x[r, g, 15, q] = 60 * k + rng.integers(0, 50, len(q))
        end = np.concatenate([late, last]); x[r, g, 0, end] = z >> 4; x[r, g, 1, end] = z & 15
        x[r, g, 15, last] = rng.integers(0, T0, WN)
        nb[r, g][:, o] = o
        sl[r, g, :, :CAP] = asked.reshape(N - 1, CAP); sl[r, g, :, G - CAP:] = late.reshape(N - 1, CAP)
        bl = np.concatenate([rng.permutation(np.repeat(np.arange(N - 1), CAP)), rng.integers(0, N - 1, WN - K)])
        nb[r, g][rng.integers(0, 16, WN), one] = aim(bl, 0)
        b = int(rng.integers(0, N - 1)); bl = rng.permutation(np.arange(L - CAP) % (N - 2))
        bl = np.concatenate([bl + (bl >= b), np.full(CAP, b)])
        nb[r, g][rng.integers(0, 16, L), np.concatenate([asked, two])] = aim(bl, G - CAP)
        wl[r, g, 0] = one; wl[r, g, 1] = two; wl[r, g, 2] = last
def setup_inputs(rng):
    return pack(*parts(rng))
def setup_inputs_room(rng):
    x, nb, pl, w, wl, sl = parts(rng); k = S // 8
    for r in range(N):
        for g in range(8):
            o = rng.permutation(S); a, b, c, e = o[:k], o[k:2 * k], o[2 * k:3 * k], o[3 * k:]
            x[r, g, 15, a] = T0 - 1; x[r, g, 0, a] = 255; x[r, g, 1, a] = 0
            x[r, g, 15, b] = 0; x[r, g, 0, b] = rng.integers(0, 255, k); x[r, g, 1, b] = rng.integers(1, 256, k)
            x[r, g, 15, c] = rng.integers(0, T0, k); x[r, g, 15, e] = -1
            for q in (a[:k // 2], b, c): nb[r, g][:, q] = q
            sl[r, g] = a[rng.integers(0, k, (N - 1, G))]
            n = rng.choice(np.array([0, 1, CAP - 1, CAP, CAP + 1]), N - 1)
            if r == 0: n[0] = (CAP, CAP + 1, CAP - 1, 0, 1, CAP + 9, CAP, CAP + 1)[g]
            else: n[rng.integers(0, N - 1)] = CAP + 9
            to = np.concatenate([S + j * G + rng.integers(0, G, int(n[j])) for j in range(N - 1)])
            go = rng.permutation(b)[:len(to)]; nb[r, g][rng.integers(0, 16, len(to)), go] = to
            wl[r, g, 0] = rng.permutation(np.concatenate([go, rng.permutation(c)[:WN - len(to)]]))
    brim(rng, x, nb, w, wl, sl, 6)
    return pack(x, nb, pl, w, wl, sl)
def setup_inputs_ties(rng):
    x, nb, pl, w, wl, sl = parts(rng); n = (N, 8, 1, S); row = np.arange(15)[:, None]
    p = 100 + (row == rng.integers(0, 22, n)).astype(np.int64) - (row == rng.integers(0, 22, n)) + (rng.random(n) < 0.1)
    x = np.concatenate([p, rng.choice(np.array([-1, -1, -1, 0, 1, 2, T0 - 2, T0 - 1]), n)], axis=2); x[:, :, 15, ::S - 1] = 0
    wl[:, :, :, 0] = 0; wl[:, :, :, 1] = S - 1; nb[:, 1::2, 8:] = nb[:, 1::2, :8]
    return pack(x, nb, pl, w, wl, sl)
def setup_inputs_crowd(rng):
    x, nb, pl, w, wl, sl = parts(rng)
    x[:, :4, :15] = np.take_along_axis(x[:, :4, :15], rng.integers(0, 8, (N, 4, 1, S)), 3)
    nb = np.where(rng.random((N, 8, 1, S)) < 0.6, np.arange(S), nb)
    w[:, 5] = 0; x[:, 5, 15][:, 97 * np.arange(RO)] = -1
    ts, zs = np.nonzero((((np.arange(Q) ** 2 >> 5) + 97 * np.arange(RO)[:, None]) & (Q - 1)) == S)
    t = int(ts[0]); z = int(zs[rng.integers(0, int(np.sum(ts == t)))])
    w[:, 7] = 0; w[:, 7, 0] = z >> 4; w[:, 7, 1] = 1
    for r in range(N):
        for g in (0, 2, 4, 6):
            few = np.concatenate([np.array([0, S - 1]), rng.integers(0, S, 10)])
            x[r, g, 15, few] = T0 - 1; nb[r, g][:, few] = few; wl[r, g] = few[rng.integers(0, 12, (RO, WN))]
        half = 1 + rng.permutation(S - 1)[:S // 2]; few = half[:8]
        x[r, 7, 0, half] = 16; x[r, 7, 1, half] = z & 15; x[r, 7, 15, 0] = -1
        x[r, 7, 15, few] = T0 - 1; nb[r, 7][:, few] = few; wl[r, 7, t, :8] = few
    return pack(x, nb, pl, w, wl, sl)
def setup_inputs_bare(rng):
    x, nb, pl, w, wl, sl = parts(rng); q = rng.permutation(N); g = rng.permutation(8)
    x[:, g[0], 15] = -1; v = x[:, g[1], 15]; x[:, g[1], 15] = np.where(v < 0, rng.integers(0, T0, v.shape), v)
    nb[:, g[3]] = rng.choice(np.array([0, S - 1, S, W - 1]), (N, 16, S)); sl[:, g[2]] = rng.choice(np.array([0, S - 1, S // 2, 3]), (N, N - 1, G))
    nb[q[0]] = rng.integers(S, W, (8, 16, S)); nb[q[1]] = rng.integers(0, S, (8, 16, S))
    return pack(x, nb, pl, w, wl, sl)
def setup_inputs_spread(rng):
    x, nb, pl, w, wl, sl = parts(rng)
    p = np.minimum((np.exp2(8 * rng.random((N, 8, 1, S))) * rng.random((N, 8, 15, S))).astype(np.int64), 255)
    st = np.minimum(np.exp2(7.6 * rng.random((N, 8, 1, S))).astype(np.int64) - 1, T0 - 1)
    st = np.where(rng.random((N, 8, 1, S)) < rng.choice(np.array([0.1, 0.4, 0.8]), (N, 8, 1, 1)), -1, st)
    w = np.minimum(np.exp2(8 * rng.random((N, 8, 16, 1))).astype(np.int64), 255)
    pl = np.minimum((np.exp2(8 * rng.random((N, 8, 1, M))) * rng.random((N, 8, 16, M))).astype(np.int64), 255)
    nb = np.where(rng.random((N, 8, 1, S)) < 0.5, rng.integers(0, W, nb.shape), nb)
    return pack(np.concatenate([p, st], axis=2), nb, pl, w, rng.integers(0, S, wl.shape), sl)
def check_inputs(d):
    bad = []
    v = np.asarray(d["x0"]).astype(np.float32).reshape(N, 8, 16, S)
    for k, a, lo, hi in (("paths of x0", v[:, :, :15], 0, 255), ("stamps of x0", v[:, :, 15], -1, T0 - 1), ("pull", np.asarray(d["pull"]).astype(np.float32), 0, 255), ("wt", d["wt"], 0, 255),
                         ("nb", d["nb"], 0, W - 1), ("wants", d["wants"], 0, S - 1), ("snd", d["snd"], 0, S - 1)):
        if not np.all((a >= lo) & (a <= hi) & (a == np.floor(a))): bad.append("range of " + k)
    return bad
def reference(x0, nb, pull, wt, wants, snd):
    x = x0.astype(np.float32).astype(np.int64).reshape(N, 8, 16, S); nbr = nb.astype(np.int64).reshape(N, 8, 16, S)
    pl = pull.astype(np.float32).astype(np.int64).reshape(N, 8, 16, M); w = wt.astype(np.int64).reshape(N, 8, 1, 16)[..., :15]
    wl = np.stack([gentries(a) for a in wants]).astype(np.int64).reshape(N, 8, RO, WN); sl = np.stack([gentries(a) for a in snd]).astype(np.int64).reshape(N, 8, N - 1, G)
    gi = np.arange(8)[:, None]; g3 = gi[:, :, None]; lane = np.arange(L)
    req = np.full((N, 8, N - 1, CAP), -1, np.int64)
    for t in range(RO):
        new = x.copy(); ask = np.full((N, 8, N - 1, CAP), -1, np.int64)
        for r in range(N):
            f = np.concatenate([x[r]] + [np.take_along_axis(x[(r - e) % N], sl[(r - e) % N, :, e - 1][:, None, :], 2) for e in range(1, N)], axis=2)
            s = np.concatenate([req[r].reshape(8, -1), wl[r, :, t]], axis=1)
            climb = s >= 0; s = np.maximum(s, 0); climb = climb & (f[gi, 15, s] >= 0); done = np.zeros((8, L), bool)
            for h in range(H):
                c = nbr[r][g3, np.arange(16), np.minimum(s, S - 1)[:, :, None]]
                a = f[g3, :, c]; b = f[gi, :, s][:, :, None, :]
                cov = (a[..., 15] > b[..., 15]) & np.any(a[..., :15] > b[..., :15], axis=3) & np.any(a[..., :15] < b[..., :15], axis=3)
                may = climb & (s < S); cov = cov & may[:, :, None]
                best = np.argmax(np.where(cov, a[..., 15], -1), axis=2)
                hit = np.any(cov, axis=2); done = done | (may & ~hit); climb = climb & hit
                s = np.where(hit, np.take_along_axis(c, best[:, :, None], 2)[:, :, 0], s)
            for e in range(1, N):
                q = (r - e) % N; k = s - S - (e - 1) * G; on = ((k >= 0) & (k < G)).astype(np.int64)
                before = np.add.accumulate(on, axis=1) - on; gs, ls = np.nonzero((on == 1) & (before < CAP))
                ask[q, gs, e - 1, before[gs, ls]] = sl[q, gs, e - 1, k[gs, ls]]
            v = f[gi, :, s]
            z = np.sum(v[:, :, :15] * w[r], axis=2) & (Q - 1); d = ((z * z >> 5) + 97 * t) & (Q - 1); d = np.where(d >= S, d - S, d)
            ok = done & (f[gi, 15, d] < 0); gs, ls = np.nonzero(ok)
            first = np.full((8, S), L, np.int64); np.minimum.at(first, (gs, d[gs, ls]), ls)
            gs, ls = np.nonzero(ok & (first[gi, d] == lane)); dd = d[gs, ls]
            new[r][gs, :15, dd] = (v[gs, ls, :15] + pl[r][gs, :15, dd & (M - 1)]) >> 1
            new[r][gs, 15, dd] = T0 + t; new[r][gs, 15, s[gs, ls]] = -1
        x = new; req = ask
    return {"y": x.reshape(N, 128, S).astype(np.float32).astype(BF)}

@@ -1,0 +1,594 @@
+from concourse.mybir import AluOpType, ActivationFunctionType
+
+S, GH, CAP, RO = 1792, 384, 32, 4
+NULL, WX, TRASH = 2944, 2960, 3072
+VL = 64
+V16 = 16 * VL
+OP = AluOpType
+AF = ActivationFunctionType
+SIZES = {
+    "bfloat16": "XT 3584,EIN 2960,PUL 512,ZSA 2048,ZSB 2048,MSK 1024,SBA 1024,SBB 1024,DA 2048,DB 2048,NA 2048,NB 2048,EXP 1024,"
+                "ONE 1024,EQ 4096,PRB 1024,IDB 128,IDN 128,EMP 128,EMN 128,GM 128,GM2 128,RD 16,RN 16,RS 384,WZ 16,DQ 256,SZA 128,"
+                "SZB 128,STA 128,STB 128,XD 256,VAL 512,STL 24,RW 192,LB 16,IND 256,CNT 256,QC 256,GS 4608,LG 4608,RG 1536,YO 1792",
+    "float32": "NBF 2960,IOT 2960,GST 2960,REQ 1280,PRF 1024,IDF 128,WM 192,COL 64,GG 64,TMF 256,TM2 512,TRS 32,TRQ 16,BSA 128,"
+               "BSB 128,TAA 128,TAB 128,MA 256,MB 256,RA 128,RB 128,KSA 64,KSB 64,DL 32,KD 128,SD 32,INV 16,TV 256,TV2 256,THE 32,"
+               "KL 128,LW 64,QX 512,RF 32,GV 256,RX 192",
+    "int32": "NBI 1792,WTI 8,WAN 40,SND 72,SNL 72,CI 32,OL 32,KIA 16,KIB 16,ZI 128,POI 32,RI 96,RSN 24",
+    "uint16": "SNU 72,SLU 72,DG 8,OFX 16,ONA 128,ONB 128,DOF 16,POF 16,DBC 256,OFS 32,RQF 16,RQO 32,RIN 32,RRQ 32",
+}
+SCRATCH = {}
+for _d, _l in SIZES.items():
+    for _x in _l.split(","):
+        SCRATCH[_x.split()[0]] = ("sbuf", [128, int(_x.split()[1])], _d)
+BANKS = ("PA", "PB", "PC0", "PC1", "PTA", "PTB", "PM", "PM2")
+for _x in BANKS:
+    SCRATCH[_x] = ("psum", [128, 512], "float32")
+SEMAPHORES = (["sV", "sS", "sP", "sG", "ls", "rs"] + ["ld%d" % i for i in range(8)] + ["st%d" % i for i in range(4)]
+              + ["ga%d_%d" % (e, t) for e in (1, 2, 3) for t in range(4)] + ["rq%d_%d" % (e, t) for e in (1, 2, 3) for t in (1, 2, 3)]
+              + ["sn%d" % e for e in (1, 2, 3)] + ["rg%d" % t for t in range(4)] + ["rr%d" % t for t in (1, 2, 3)])
+
+
+def routes(T, topo):
+    n = len(T.cores)
+    rel = {}
+    for r in range(n):
+        c = T.cores[r]
+        near = True
+        for e in range(1, n):
+            d = (r + e) % n
+            if topo.may_write(c, T.cores[d]):
+                rel[(r, d)] = None
+                continue
+            cand = [k for k in topo.cores_of(c) if k != c and topo.may_write(k, T.cores[d]) and topo.may_write(c, k)]
+            pick = [k for k in cand if (topo.die(k) == topo.die(c)) == near] or cand
+            rel[(r, d)] = pick[0]
+            near = False
+    return rel
+
+
+def count(m):
+    return bin(m).count("1")
+
+
+def relay_program(g, core, T, topo, r, d):
+    n = len(T.cores)
+    src, dst = T.cores[r], T.cores[d]
+    e, eq = (d - r) % n, (r - d) % n
+    k_in, m = count(topo.mask(src, core)), topo.mask(core, dst)
+    rid, pid = topo.addr(dst, core)
+
+    def on(sem, out, in_, rsem):
+        g.wait_ge(T.sem[sem], k_in)
+        g.remote_dma(out, in_, T.sem[rsem], T.sem["ls"], pid, rid, m)
+    for t in range(RO):
+        on("rg%d" % t, T["LG"][:, t * 1152 + (e - 1) * GH:t * 1152 + e * GH], T["RG"][:, t * GH:(t + 1) * GH], "ga%d_%d" % (e, t))
+        if t == 0:
+            on("rs", T["SNL"][:, (e - 1) * 24:e * 24], T["RSN"][:, 0:24], "sn%d" % e)
+        else:
+            on("rr%d" % t, T["RIN"][:, t * 8 + 2 * (eq - 1):t * 8 + 2 * eq], T["RRQ"][:, t * 8:t * 8 + 2], "rq%d_%d" % (eq, t))
+    g.wait_ge(T.sem["ls"], 2 * RO * count(m))
+
+
+def rank_program(g, core, T, topo):
+    rel = routes(T, topo)
+    rank = T.rank_of(core)
+    if rank is None:
+        for (r, d), k in rel.items():
+            if k == core:
+                relay_program(g, core, T, topo, r, d)
+        return
+    n = len(T.cores)
+    queue = {"V": g.vector, "S": g.scalar, "P": g.tensor, "G": g, "Y": g.sync}
+    clock = {k: {} for k in queue}
+    total = {}
+    acc = {}
+
+    def need(q, ev, ck):
+        s, v = ev
+        if clock[q].get(s, 0) < v:
+            queue[q].wait_ge(T.sem[s], v)
+            clock[q][s] = v
+        for a, b in ck.items():
+            if clock[q].get(a, 0) < b:
+                clock[q][a] = b
+
+    def span(s):
+        return (s[0], 0, 512) if s[0] in BANKS else (s[0], s[1], s[2])
+
+    def before(q, reads, writes):
+        todo = []
+        for w, lst in ((False, reads), (True, writes)):
+            for s in lst:
+                b, lo, hi = span(s)
+                for a in acc.get(b, []):
+                    if a[0] < hi and lo < a[1]:
+                        if not w and not a[2] and not (b in BANKS and a[3] != q):
+                            continue
+                        if a[3] == q and (w or b in BANKS and q == "P"):
+                            continue
+                        todo.append((a[4], a[5]))
+        todo.sort(key=lambda x: -x[0][1])
+        for ev, ck in todo:
+            if clock[q].get(ev[0], 0) < ev[1]:
+                need(q, ev, ck)
+
+    def after(q, ev, reads, writes, by):
+        ck = dict(clock[by])
+        for w, lst in ((False, reads), (True, writes)):
+            for s in lst:
+                b, lo, hi = span(s)
+                old = acc.setdefault(b, [])
+                if w and len(s) < 4:
+                    old[:] = [a for a in old if not (lo <= a[0] and a[1] <= hi)]
+                elif not w:
+                    old[:] = [a for a in old if a[2] or a[3] != q or not (lo <= a[0] and a[1] <= hi)]
+                old.append([lo, hi, w, q, ev, ck])
+
+    def do(q, fn, reads, writes):
+        before(q, reads, writes)
+        s = "s" + q
+        total[s] = total.get(s, 0) + 1
+        fn(queue[q]).then_inc(T.sem[s], 1)
+        after(q, (s, total[s]), reads, writes, q)
+
+    def dma(q, sem, out, in_, reads, writes):
+        before(q, reads, writes)
+        total[sem] = total.get(sem, 0) + 16
+        queue[q].dma_start(out, in_).then_inc(T.sem[sem], 16)
+        after(sem, (sem, total[sem]), reads, writes, q)
+
+    def lands(s, sem, k):
+        total[sem] = total.get(sem, 0) + k
+        acc.setdefault(s[0], []).append([s[1], s[2], True, "remote", (sem, total[sem]), {}])
+
+    def ap(s):
+        if s[0] == "I":
+            return ap(s[1]).indirect(ap(s[2]))
+        return T[s[0]][:, s[1]:s[2]] if len(s) == 3 else T[s[0]][:, s[1]:s[2]:s[3]]
+
+    def rd(*ss):
+        out = []
+        for s in ss:
+            if isinstance(s, tuple):
+                out += [s[1], s[2]] if s[0] == "I" else [s]
+        return out
+
+    def wr(s):
+        return [s[1]] if s[0] == "I" else [s]
+
+    def val(s):
+        return ap(s) if isinstance(s, tuple) else s
+
+    def tt(out, a, b, op):
+        do("V", lambda v: v.tensor_tensor(ap(out), ap(a), ap(b), op), rd(a, b), wr(out))
+
+    def ts(out, a, s1, op0, s2=None, op1=None):
+        if op1 is None:
+            do("V", lambda v: v.tensor_scalar(ap(out), ap(a), val(s1), None, op0), rd(a, s1), wr(out))
+        else:
+            do("V", lambda v: v.tensor_scalar(ap(out), ap(a), val(s1), val(s2), op0, op1), rd(a, s1, s2), wr(out))
+
+    def cp(out, a):
+        do("V", lambda v: v.tensor_copy(ap(out), ap(a)), rd(a) + (rd(out)[1:] if out[0] == "I" else []), wr(out))
+
+    def scan(out, d0, d1, op0, op1):
+        do("V", lambda v: v.tensor_tensor_scan(ap(out), ap(d0), ap(d1), 0.0, op0, op1), rd(d0, d1), wr(out))
+
+    def fill(out, c):
+        do("V", lambda v: v.memset(ap(out), c), [], wr(out))
+
+    def act(out, a, func=AF.Copy, **kw):
+        do("S", lambda s: s.activation(ap(out), ap(a), func, **{k: val(x) for k, x in kw.items()}), rd(a, *kw.values()), wr(out))
+
+    def mm(out, l, r, start, stop):
+        do("P", lambda p: p.matmul(ap(out), ap(l), ap(r), start, stop), rd(l, r), wr(out))
+
+    def iota(out, pat, base=0, cm=0):
+        kw = {} if SCRATCH[out[0]][2] == "int32" else {"allow_small_or_imprecise_dtypes": True}
+        do("G", lambda q: q.iota(ap(out), pat, base, cm, **kw), [], wr(out))
+
+    def pick(out, a, pat, base):
+        do("G", lambda q: q.affine_select(ap(out), ap(a), pat, OP.is_equal, 0.0, base, 1), rd(a), wr(out))
+
+    def send(in_, d, kind, e, t):
+        k = rel[(rank, d)]
+        before("G", [in_], [])
+        if k is None:
+            out, sem = {"g": (("LG", t * 1152 + (e - 1) * GH), "ga%d_%d" % (e, t)), "s": (("SNL", (e - 1) * 24), "sn%d" % e),
+                        "q": (("RIN", t * 8 + 2 * (e - 1)), "rq%d_%d" % (e, t))}[kind]
+        else:
+            out, sem = {"g": (("RG", t * GH), "rg%d" % t), "s": (("RSN", 0), "rs"), "q": (("RRQ", t * 8), "rr%d" % t)}[kind]
+        to = T.cores[d] if k is None else k
+        rid, pid = topo.addr(to, core)
+        m = topo.mask(core, to)
+        g.remote_dma(T[out[0]][:, out[1]:out[1] + in_[2] - in_[1]], ap(in_), T.sem[sem], T.sem["ls"], pid, rid, m)
+        total["ls"] = total.get("ls", 0) + count(m)
+
+    def due(d):
+        k = rel[(d, rank)]
+        return count(topo.mask(T.cores[d] if k is None else k, core))
+
+    def col(i):
+        return ("COL", i, i + 1)
+
+    def ci(i):
+        return ("CI", i, i + 1)
+
+    QF, GF, N15, I15, SC, B1, HLF, THR, QP, TMPC, KB = [col(i) for i in range(11)]
+    NVB = [col(12 + i) for i in range(4)]
+    WIN, OWN, NBW = ("XT", 0, WX), ("XT", 0, S), ("NBF", 0, WX)
+    GM, GG = ("GM", 0, 128), ("GG", 0, 8)
+
+    dma("Y", "ld0", T["XT"][:, 0:S], T.x0[:, :], [], [OWN])
+    dma("S", "ld1", T["SND"][:, :], T.snd[:, :], [], [("SND", 0, 72)])
+    dma("Y", "ld2", T["NBI"][:, :], T.nb[:, :], [], [("NBI", 0, S)])
+    dma("S", "ld3", T["WAN"][:, :], T.wants[:, :], [], [("WAN", 0, 40)])
+    dma("S", "ld4", T["WTI"][:, 0:1], T.wt[:, :], [], [("WTI", 0, 1)])
+    dma("S", "ld5", T["PUL"][:, :], T.pull[:, :], [], [("PUL", 0, 512)])
+
+    iota(ci(0), [[1, 1]], 0, 1)
+    iota(("TMF", 0, 128), [[1, 8], [0, 16]])
+    iota(("TM2", 0, 128), [[0, 8], [1, 16]])
+    iota(GG, [[1, 8]])
+    iota(("QX", 0, 256), [[1, 16], [0, 16]])
+    iota(("MSK", 0, 1024), [[0, 64], [1, 16]])
+    fill(("ONE", 0, 1024), 1.0)
+    pick(("IDB", 0, 128), ("ONE", 0, 128), [[-1, 128]], 0)
+    fill(("XT", NULL, WX), 0.0)
+    ts(ci(1), ci(0), 15, OP.bitwise_and)
+    ts(ci(2), ci(0), 4, OP.logical_shift_right)
+    cp(QF, ci(1))
+    cp(GF, ci(2))
+    ts(N15, QF, 15.0, OP.is_lt)
+    ts(I15, QF, 15.0, OP.is_equal)
+    ts(TMPC, I15, -256.0, OP.mult)
+    ts(GM, ("TMF", 0, 128), GF, OP.is_equal)
+    ts(("TM2", 0, 128), ("TM2", 0, 128), 15.0, OP.is_lt)
+    tt(("TM2", 0, 128), ("TM2", 0, 128), GM, OP.mult)
+    ts(("EMP", 0, 128), ("TM2", 0, 128), TMPC, OP.mult)
+    ts(("EMN", 0, 128), ("EMP", 0, 128), -1.0, OP.mult)
+    cp(("SNU", 0, 72), ("SND", 0, 72))
+    for x in "AB":
+        for k in (0, 1024):
+            act(("ZS" + x, k, k + 1024), ("ONE", 0, 1024), AF.Identity, scale=0.0)
+        act(("SZ" + x, 0, 128), ("ONE", 0, 128), AF.Identity, scale=0.0)
+    fill(("OL", 0, 32), 0)
+    ts(GG, GG, GF, OP.is_equal)
+    ts(("RD", 0, 8), GG, N15, OP.mult, 16777216.0, OP.mult)
+    ts(("RD", 8, 16), GG, I15, OP.mult, 69632.0, OP.mult)
+    cp(("RN", 0, 8), ("RD", 0, 8))
+    cp(("RN", 8, 16), ("RD", 0, 8))
+    ts(col(16), N15, -16777216.0, OP.mult)
+    ts(col(17), I15, -69632.0, OP.mult)
+    ts(col(18), GF, 8.0, OP.add)
+    ts(("TM2", 0, 256), ("QX", 0, 256), GF, OP.is_equal, col(16), OP.mult)
+    ts(("TM2", 256, 512), ("QX", 0, 256), col(18), OP.is_equal, col(17), OP.mult)
+    fill(("RS", 0, 128), 0.0)
+    tt(("RS", 128, 384), ("TM2", 0, 256), ("TM2", 256, 512), OP.add)
+    cp(("IDF", 0, 128), ("IDB", 0, 128))
+    ts(("IDN", 0, 128), ("IDB", 0, 128), -1.0, OP.mult)
+    ts(ci(3), ci(1), 7, OP.bitwise_and)
+    ts(ci(4), ci(1), 3, OP.logical_shift_right)
+    ts(col(19), ci(3), 8.0, OP.mult)
+    ts(col(20), ci(4), 8.0, OP.mult)
+    tt(col(21), col(19), GF, OP.add)
+    tt(col(22), col(21), col(19), OP.add)
+    tt(col(23), col(22), col(20), OP.add)
+    cp(("DG", 0, 1), col(21))
+    cp(("DG", 2, 3), col(23))
+    cp(("DG", 3, 4), col(23))
+    ban = ["PC0", "PC1", "PTA", "PTB"]
+    part = [(448 * k, 448 * (k + 1)) for k in range(4)]
+    for k, (a, b) in enumerate(part):
+        ts(("YO", a, b), ("XT", a, b), 0.0, OP.is_lt)
+        mm((ban[k], 0, 448), ("EMP", 0, 128), ("YO", a, b), True, True)
+    for k, (a, b) in enumerate(part):
+        tt(("XT", a, b), ("XT", a, b), (ban[k], 0, 448), OP.add)
+
+    def ghosts(t):
+        at = t * 1152
+        act(("GS", at, at + 384), ("I", OWN, ("SNU", 0, 24)))
+        cp(("GS", at + 768, at + 1152), ("I", OWN, ("SNU", 48, 72)))
+        send(("GS", at, at + 384), (rank + 1) % n, "g", 1, t)
+        send(("GS", at + 768, at + 1152), (rank + 3) % n, "g", 3, t)
+        act(("GS", at + 384, at + 576), ("I", OWN, ("SNU", 24, 36)))
+        cp(("GS", at + 576, at + 768), ("I", OWN, ("SNU", 36, 48)))
+        send(("GS", at + 384, at + 768), (rank + 2) % n, "g", 2, t)
+        for e in (1, 2, 3):
+            lands(("LG", at + (e - 1) * GH, at + e * GH), "ga%d_%d" % (e, t), due((rank - e) % n))
+
+    ghosts(0)
+    for e in (1, 3, 2):
+        send(("SND", (e - 1) * 24, e * 24), (rank + e) % n, "s", e, 0)
+        lands(("SNL", (e - 1) * 24, e * 24), "sn%d" % e, due((rank - e) % n))
+
+    iota(("IOT", 0, WX), [[1, WX]])
+    pick(("EXP", 0, 2048 - V16), ("ONE", 0, 2048 - V16), [[-1, 128 - VL], [0, 16]], -VL)
+    pick(("PRB", 0, 1024), ("ONE", 0, 1024), [[-16, 8], [0, 8], [-1, 16]], 0)
+    iota(("TMF", 0, 256), [[0, 16], [1, 16]])
+    iota(("TRS", 0, 32), [[16, 32]], TRASH)
+    iota(("TRQ", 0, 16), [[16, 16]], 1024)
+    for b, lo, hi in (("EIN", 0, S), ("EIN", NULL, WX), ("GST", 0, S), ("GST", NULL, WX), ("EQ", 0, 4096), ("REQ", 0, 1280)):
+        iota((b, lo, hi), [[0, hi - lo]])
+    ts(KB, QF, 1.0, OP.add, -4096.0, OP.mult)
+    ts(("MSK", 0, 1024), ("MSK", 0, 1024), 0.5, OP.is_gt)
+    cp(("NBF", 0, S), ("NBI", 0, S))
+    act(("NBF", S, WX), ("IOT", S, WX))
+    ts(("WZ", 8, 16), GG, I15, OP.mult)
+    cp(SC, N15)
+    ts(B1, N15, -255.0, OP.mult, -1.0, OP.add)
+    ts(HLF, N15, 0.5, OP.mult)
+    ts(col(24), N15, -8388608.0, OP.mult)
+    for t in range(RO):
+        ts(NVB[t], I15, float(192 + t), OP.mult, col(24), OP.add)
+    fill(QP, 32768.0)
+    for k in range(4):
+        ts(ci(8), ci(1), k, OP.logical_shift_right, 1, OP.bitwise_and)
+        ts(col(25), ci(8), 2.0 ** -(2 ** k) - 1.0, OP.mult, 1.0, OP.add)
+        tt(QP, QP, col(25), OP.mult)
+    for c in range(8):
+        w = 2.0 ** (17 * (7 - c) - 44)
+        ts(("WM", c * 24, c * 24 + 8), GG, QP, OP.mult, w, OP.mult)
+        ts(("WM", c * 24 + 8, c * 24 + 16), GG, QP, OP.mult, w, OP.mult)
+        ts(("WM", c * 24 + 16, c * 24 + 24), GG, 2.0 ** 92, OP.mult)
+        fill(("GG", 16 + c, 17 + c), 2.0 * w)
+    tt(("GG", 32, 40), GG, ("GG", 16, 24), OP.mult)
+    tt(("GG", 32, 36), ("GG", 32, 36), ("GG", 36, 40), OP.add)
+    tt(("GG", 32, 34), ("GG", 32, 34), ("GG", 34, 36), OP.add)
+    tt(col(26), ("GG", 32, 33), ("GG", 33, 34), OP.add)
+    tt(THR, col(26), QP, OP.mult)
+    ts(col(27), QF, 1.0, OP.add, 512.0, OP.mult)
+    ts(("GM2", 0, 128), GM, col(27), OP.mult)
+    act(("PRF", 0, 1024), ("PRB", 0, 1024))
+
+    def later_consts():
+        ts(("DQ", 0, 256), ("TMF", 0, 256), QF, OP.is_equal)
+        ts(("TRS", 0, 32), ("TRS", 0, 32), QF, OP.add)
+        ts(("TRQ", 0, 16), ("TRQ", 0, 16), QF, OP.add)
+        cp(TMPC, ("WTI", 0, 1))
+        ts(("WZ", 0, 8), GG, TMPC, OP.mult, N15, OP.mult)
+        for e in (1, 2, 3):
+            lo = S + (e - 1) * GH
+            ts(col(27 + e), QF, float(e - 1), OP.is_equal)
+            act(("EIN", lo, lo + GH), ("IOT", lo, lo + GH), AF.Identity, scale=0.0, bias=col(27 + e))
+        for e in (2, 1, 3):
+            lo = S + (e - 1) * GH
+            cp(("SLU", (e - 1) * 24, e * 24), ("SNL", (e - 1) * 24, e * 24))
+            act(("GST", lo, lo + GH), ("I", ("IOT", 0, S), ("SLU", (e - 1) * 24, e * 24)))
+
+    O8 = {"A": 0, "B": 8}
+
+    def OFX(x, a, b):
+        return ("OFX", O8[x] + a, O8[x] + b)
+
+    def OLD(x, a, b):
+        return ("OL", 2 * O8[x] + a, 2 * O8[x] + b)
+
+    def start_b(t):
+        cp(OLD("B", 0, 8), ("WAN", t * 10 + 2, t * 10 + 10))
+        cp(OFX("B", 0, 8), OLD("B", 0, 8))
+
+    def start_a(t):
+        cp(OLD("A", 6, 8), ("WAN", t * 10, t * 10 + 2))
+        if t == 0:
+            fill(OLD("A", 0, 6), NULL)
+        else:
+            cp(OLD("A", 0, 6), ("RIN", t * 8, t * 8 + 6))
+        cp(OFX("A", 0, 8), OLD("A", 0, 8))
+
+    def own_v(x, win):
+        cp(("ON" + x, 0, 128), ("I", NBW, OFX(x, 0, 8)))
+        cp(("ZS" + x, 0, V16, 16), ("I", win, OFX(x, 0, VL // 16)))
+        scan(("SB" + x, 0, V16), ("MSK", 0, V16), ("ZS" + x, 0, V16), OP.mult, OP.add)
+
+    def own_s(x, win):
+        act(("SZ" + x, VL, 128), ("I", win, OFX(x, VL // 16, 8)))
+        mm(("PT" + x, 128, 256), ("SZ" + x, 0, 128), ("IDN", 0, 128), True, True)
+        act(("BS" + x, 0, 128), ("I", NBW, OFX(x, 0, 8)), AF.Identity, bias=KB)
+        mm(("P" + x, 0, 384), ("SZ" + x, 0, 128), ("RS", 0, 384), True, False)
+        mm(("P" + x, 256, 384), ("BS" + x, 0, 128), ("IDF", 0, 128), False, False)
+
+    def own_t(x):
+        act(("ST" + x, 0, 128), ("PT" + x, 128, 256))
+
+    def big_s(x, k):
+        a, pc = V16 + 512 * k, ("PC%d" % k, 0, 512)
+        act(("D" + x, a, a + 512), ("I", WIN, ("ON" + x, a // 16, a // 16 + 32)))
+        mm(pc, ("IDB", 0, 128), ("D" + x, a, a + 512), True, False)
+        mm(pc, ("ST" + x, 0, 128), ("EXP", 512 * k, 512 * k + 512), False, True)
+
+    def relu(x, k):
+        a = V16 + 512 * k
+        act(("N" + x, a, a + 512), ("PC%d" % k, 0, 512), AF.Relu, scale=-1.0)
+
+    def sums(ps, buf, rhs, lo, stop):
+        for i in range(16):
+            mm((ps, lo + i, lo + 256, 16), (buf, i, 2048, 16), (rhs, 0, 16), False, stop and i == 15)
+
+    def best(x):
+        ps, m = "P" + x, "M" + x
+        cp(("TA" + x, 0, 128), (ps, 0, 128))
+        tt((m, 0, 128), ("TA" + x, 0, 128), (ps, 128, 256), OP.min)
+        tt((m, 128, 256), (m, 0, 128), (ps, 256, 384), OP.min)
+        scan(("R" + x, 0, 128), ("MSK", 0, 128), (m, 128, 256), OP.mult, OP.max)
+
+    def turn(ps, w, mat, rhs):
+        for c in range(8):
+            mm((ps, c * w, c * w + w), (mat, c * 128, c * 128 + 128), rhs, True, True)
+
+    def perm(x):
+        turn("PT" + x, 8, "PRF", ("R" + x, 15, 128, 16))
+
+    def step(x):
+        cp(("KS" + x, 0, 64), ("PT" + x, 0, 64))
+        tt(("KI" + x, 0, 16), ("I", ("KS" + x, 0, 64), ("DG", 0, 1)), OLD(x, 0, 16), OP.max)
+        ts(OLD(x, 0, 16), ("KI" + x, 0, 16), 4095, OP.bitwise_and)
+        cp(OFX(x, 0, 8), OLD(x, 0, 8))
+
+    def places_p():
+        for b, x in enumerate("AB"):
+            for k in (0, 8):
+                o = ("PM", 2 * k + 8 * b, 2 * k + 8 * b + 8)
+                mm(o, ("ZS" + x, 0, 2048, 16), ("WZ", k, k + 8), True, False)
+                mm(o, ("SZ" + x, 0, 128), ("WZ", k, k + 8), False, True)
+
+    def places(t):
+        z = [("ZI", 16 * i, 16 * i + 16) for i in range(8)]
+        ts(("DL", 16, 32), ("PM", 16, 32), 0.0, OP.is_lt, float(NULL), OP.mult)
+        cp(z[0], ("PM", 0, 16))
+        ts(z[1], z[0], 2047, OP.bitwise_and)
+        tt(z[2], z[1], z[1], OP.mult)
+        ts(z[3], z[2], float(97 * t * 32), OP.add)
+        ts(z[4], z[3], 5, OP.logical_shift_right, 2047, OP.bitwise_and)
+        ts(z[5], z[4], float(S), OP.is_ge, -float(S), OP.mult)
+        tt(z[6], z[4], z[5], OP.add)
+        tt(("DL", 0, 16), z[6], ("DL", 16, 32), OP.max)
+        turn("PM2", 16, "PRF", ("DL", 0, 16))
+        for k, x in ((0, "A"), (8, "B")):
+            ts(("INV", k, k + 8), OLD(x, 0, 8), float(S), OP.is_ge, float(NULL), OP.mult)
+            cp(("SD", 16 + k, 24 + k), OLD(x, 0, 8))
+
+    def places2():
+        cp(("KD", 0, 128), ("PM2", 0, 128))
+        tt(("SD", 0, 16), ("I", ("KD", 0, 128), ("DG", 2, 3)), ("INV", 0, 16), OP.max)
+        cp(("DOF", 0, 16), ("SD", 0, 16))
+        cp(("DBC", 0, 256), ("I", ("IOT", 0, WX), ("DOF", 0, 16)))
+
+    def places3():
+        for c in range(16):
+            ts(("EQ", c * 272, c * 256 + 256), ("DBC", 16 * c, 256), ("SD", c, c + 1), OP.is_equal)
+
+    def places4():
+        cp(("POI", 0, 16), ("SD", 0, 16))
+        ts(("POI", 16, 32), ("POI", 0, 16), 511, OP.bitwise_and)
+        cp(("POF", 0, 16), ("POI", 16, 32))
+        for o, x in ((0, "A"), (128, "B")):
+            p, q = o // 16, (o + VL) // 16
+            tt(("TV", o, o + VL), ("I", ("PUL", 0, 512), ("POF", p, q)), ("ZS" + x, 0, V16, 16), OP.add)
+            tt(("TV", o + VL, o + 128), ("I", ("PUL", 0, 512), ("POF", q, p + 8)), ("SZ" + x, VL, 128), OP.add)
+        ts(("TV2", 0, 256), ("TV", 0, 256), -0.5, OP.add, 16777216.0, OP.add)
+
+    def places_s():
+        act(("XD", 0, 256), ("I", WIN, ("DOF", 0, 16)))
+        for b in (0, 1):
+            mm(("PM", 32 + 8 * b, 40 + 8 * b), ("XD", 128 * b, 128 * b + 128), ("WZ", 8, 16), True, True)
+        for o, x in ((256, "A"), (384, "B")):
+            act(("VAL", o, o + VL), ("ZS" + x, 0, V16, 16), AF.Identity, scale=SC, bias=B1)
+            act(("VAL", o + VL, o + 128), ("SZ" + x, VL, 128), AF.Identity, scale=SC, bias=B1)
+
+    def moves(t):
+        for k, x in ((0, "A"), (8, "B"), (16, "A")):
+            ts(("STL", k, k + 8), ("R" + x, 15, 128, 16), 0.0, OP.is_equal)
+        turn("PM2", 24, "PRB", ("STL", 0, 24))
+        ts(("THE", 0, 16), ("PM", 32, 48), 0.0, OP.is_lt, THR, OP.mult)
+        tt(("THE", 16, 32), ("THE", 0, 16), ("STL", 0, 16), OP.mult)
+        tt(("RW", 0, 192), ("PM2", 0, 192), ("WM", 0, 192), OP.mult)
+        for c in range(8):
+            mm(("PM", 0, 8), ("EQ", c * 256, c * 256 + 128), ("RW", c * 24, c * 24 + 8), c == 0, c == 7)
+        for c in range(16):
+            o = (c % 8) * 24 + (8 if c >= 8 else 16)
+            mm(("PM", 8, 16), ("EQ", c * 256 + 128, c * 256 + 256), ("RW", o, o + 8), c == 0, c == 15)
+        places4()
+        act(("VAL", 0, 256), ("TV2", 0, 256), AF.Identity, scale=HLF, bias=NVB[t])
+        tt(("LB", 0, 16), ("PM", 0, 16), ("THE", 16, 32), OP.is_ge)
+        turn("PM2", 16, "PRB", ("LB", 0, 16))
+        cp(("KL", 0, 128), ("PM2", 0, 128))
+        tt(("LW", 0, 32), ("I", ("KL", 0, 128), ("DG", 2, 4)), ("TRS", 0, 32), OP.mult)
+        tt(("LW", 32, 64), ("LW", 0, 32), ("SD", 0, 32), OP.max)
+        cp(("OFS", 0, 32), ("LW", 32, 64))
+        cp(("I", ("XT", 0, 3584), ("OFS", 0, 32)), ("VAL", 0, 512))
+
+    def requests(t):
+        act(("GV", 0, 256), ("I", ("GST", 0, WX), ("OFX", 0, 16)))
+        cp(("IND", 0, 256), ("I", ("EIN", 0, WX), ("OFX", 0, 16)))
+        scan(("CNT", 0, 256), ("ONE", 0, 256), ("IND", 0, 256), OP.mult, OP.add)
+        tt(("QC", 0, 256), ("IND", 0, 256), ("CNT", 0, 256), OP.mult)
+        mm(("PC0", 0, 256), ("GM2", 0, 128), ("IND", 0, 256), True, False)
+        mm(("PC0", 0, 256), GM, ("QC", 0, 256), False, True)
+        fill(("REQ", 32, 128), float(NULL))
+        tt(("QX", 0, 256), ("PC0", 0, 256), ("DQ", 0, 256), OP.mult)
+        scan(("QX", 256, 512), ("MSK", 0, 256), ("QX", 0, 256), OP.mult, OP.add)
+        r = [("RI", 16 * i, 16 * i + 16) for i in range(6)]
+        ts(r[0], ("QX", 271, 512, 16), -1.0, OP.add)
+        ts(r[1], r[0], 511, OP.bitwise_and)
+        ts(r[2], r[0], 4, OP.arith_shift_right, 96, OP.bitwise_and)
+        ts(("RF", 0, 16), r[1], float(CAP), OP.is_ge)
+        tt(r[3], r[1], r[2], OP.add)
+        tt(("RF", 16, 32), ("RF", 0, 16), ("TRQ", 0, 16), OP.mult)
+        tt(r[4], r[3], ("RF", 16, 32), OP.max)
+        cp(("RQF", 0, 16), r[4])
+        cp(("I", ("REQ", 0, 1280), ("RQF", 0, 16)), ("GV", 0, 256))
+        tt(("RX", 0, 96), ("REQ", 32, 128), ("DQ", 0, 96), OP.mult)
+        scan(("RX", 96, 192), ("MSK", 0, 96), ("RX", 0, 96), OP.mult, OP.add)
+        o = (t + 1) * 8
+        cp(("RQO", o, o + 6), ("RX", 111, 192, 16))
+        for e in (1, 3, 2):
+            send(("RQO", o + 2 * (e - 1), o + 2 * e), (rank - e) % n, "q", e, t + 1)
+            lands(("RIN", o + 2 * (e - 1), o + 2 * e), "rq%d_%d" % (e, t + 1), due((rank + e) % n))
+
+    order = [("B", 0), ("A", 0), ("B", 1), ("A", 1), ("B", 2), ("A", 2)]
+    for t in range(RO):
+        start_b(t)
+        own_s("B", OWN)
+        own_t("B")
+        own_v("B", OWN)
+        for e in (2, 1, 3):
+            lo = (e - 1) * GH
+            act(("XT", S + lo, S + lo + GH), ("LG", t * 1152 + lo, t * 1152 + lo + GH))
+        for i, (x, h) in enumerate(order):
+            y = "B" if x == "A" else "A"
+            last = i == 5
+            big_s(x, 0)
+            if i:
+                best(y)
+                if not last:
+                    perm(y)
+            if last:
+                places_p()
+            big_s(x, 1)
+            if last:
+                places(t)
+            big = ("D" + x, 0, V16)
+            tt(big, ("I", WIN, ("ON" + x, 0, VL)), ("SB" + x, 0, V16), OP.subtract)
+            if i and not last:
+                step(y)
+            if i == 0:
+                start_a(t)
+            if last:
+                places2()
+            relu(x, 0)
+            sums("P" + x, "D" + x, "RD", 128, False)
+            if not last:
+                own_s(y, WIN)
+            relu(x, 1)
+            ts(("N" + x, 0, V16), big, -1.0, OP.mult, 0.0, OP.max)
+            sums("P" + x, "N" + x, "RN", 0, True)
+            if not last:
+                own_t(y)
+                own_v(y, WIN)
+            if t == 0 and i == 3:
+                later_consts()
+        places3()
+        places_s()
+        best("A")
+        moves(t)
+        if t + 1 < RO:
+            ghosts(t + 1)
+            perm("B")
+            perm("A")
+            step("B")
+            step("A")
+            requests(t)
+
+    for k, (a, b) in enumerate(part):
+        ts(("DB", a, b), ("XT", a, b), 0.0, OP.is_lt)
+        mm((ban[k], 0, 448), ("IDB", 0, 128), ("XT", a, b), True, False)
+        mm((ban[k], 0, 448), ("EMN", 0, 128), ("DB", a, b), False, True)
+        if k % 2:
+            cp(("YO", a, b), (ban[k], 0, 448))
+        else:
+            act(("YO", a, b), (ban[k], 0, 448))
+        dma("Y", "st%d" % k, T.y[:, a:b], T["YO"][:, a:b], [("YO", a, b)], [])
+    for s in sorted(total):
+        if clock["G"].get(s, 0) < total[s]:
+            g.wait_ge(T.sem[s], total[s])

@@ -9,11 +9,12 @@ AF = ActivationFunctionType
 SIZES = {
     "bfloat16": "XT 3584,EIN 2960,PUL 512,ZSA 2048,ZSB 2048,MSK 1024,SBA 1024,SBB 1024,DA 2048,DB 2048,NA 2048,NB 2048,EXP 1024,"
                 "ONE 1024,EQ 4096,PRB 1024,IDB 128,IDN 128,EMP 128,EMN 128,GM 128,GM2 128,RD 16,RN 16,RS 384,WZ 16,DQ 256,SZA 128,"
-                "SZB 128,STA 128,STB 128,XD 256,VAL 512,STL 24,RW 192,LB 16,IND 256,CNT 256,QC 256,GS 4608,LG 4608,RG 1536,YO 1792",
-    "float32": "NBF 2960,IOT 2960,GST 2960,REQ 1280,PRF 1024,IDF 128,WM 192,COL 64,GG 64,TMF 256,TM2 512,TRS 32,TRQ 16,BSA 128,"
+                "SZB 128,STA 128,STB 128,XD 256,VAL 512,STL 24,RW 192,LB 16,IND 256,CNT 256,QC 256,GS 4608,LG 4608,RG 1536,YO 1792,"
+                "REB 128",
+    "float32": "NBF 2960,IOT 2960,GST 2960,REQ 2320,PRF 1024,IDF 128,WM 192,COL 64,GG 64,TMF 256,TM2 512,TRS 32,BSA 128,"
                "BSB 128,TAA 128,TAB 128,MA 256,MB 256,RA 128,RB 128,KSA 64,KSB 64,DL 32,KD 128,SD 32,INV 16,TV 256,TV2 256,THE 32,"
-               "KL 128,LW 64,QX 512,RF 32,GV 256,RX 192",
-    "int32": "NBI 1792,WTI 8,WAN 40,SND 72,SNL 72,CI 32,OL 32,KIA 16,KIB 16,ZI 128,POI 32,RI 96,RSN 24",
+               "KL 128,LW 64,QX 512,GV 256,RX 192,REP 128,KQA 64,KQB 64",
+    "int32": "NBI 1792,WTI 8,WAN 40,SND 72,SNL 72,CI 32,OL 32,KIA 16,KIB 16,ZI 128,POI 32,RSN 24",
     "uint16": "SNU 72,SLU 72,DG 8,OFX 16,ONA 128,ONB 128,DOF 16,POF 16,DBC 256,OFS 32,RQF 16,RQO 32,RIN 32,RRQ 32",
 }
 SCRATCH = {}
@@ -82,6 +83,7 @@ def rank_program(g, core, T, topo):
     clock = {k: {} for k in queue}
     total = {}
     acc = {}
+    tape = [None]
 
     def need(q, ev, ck):
         s, v = ev
@@ -125,11 +127,33 @@ def rank_program(g, core, T, topo):
                 old.append([lo, hi, w, q, ev, ck])
 
     def do(q, fn, reads, writes):
+        if tape[0] is not None:
+            tape[0].append((q, fn, reads, writes))
+            return
         before(q, reads, writes)
         s = "s" + q
         total[s] = total.get(s, 0) + 1
         fn(queue[q]).then_inc(T.sem[s], 1)
         after(q, (s, total[s]), reads, writes, q)
+
+    def rec(f, *args):
+        tape[0] = []
+        f(*args)
+        out, tape[0] = tape[0], None
+        return out
+
+    def weave(a, b, pat):
+        lists = {"a": a[:], "b": b[:]}
+        for c in pat + "a" * len(a) + "b" * len(b):
+            lst = lists[c]
+            seen = False
+            while lst and not (seen and lst[0][0] == "V"):
+                seen = seen or lst[0][0] == "V"
+                x = lst.pop(0)
+                if x[0] == "send":
+                    send(*x[1])
+                else:
+                    do(*x)
 
     def dma(q, sem, out, in_, reads, writes):
         before(q, reads, writes)
@@ -144,6 +168,8 @@ def rank_program(g, core, T, topo):
     def ap(s):
         if s[0] == "I":
             return ap(s[1]).indirect(ap(s[2]))
+        if len(s) == 5:
+            return T[s[0]][0:s[4], s[1]:s[2]]
         return T[s[0]][:, s[1]:s[2]] if len(s) == 3 else T[s[0]][:, s[1]:s[2]:s[3]]
 
     def rd(*ss):
@@ -191,6 +217,9 @@ def rank_program(g, core, T, topo):
         do("G", lambda q: q.affine_select(ap(out), ap(a), pat, OP.is_equal, 0.0, base, 1), rd(a), wr(out))
 
     def send(in_, d, kind, e, t):
+        if tape[0] is not None:
+            tape[0].append(("send", (in_, d, kind, e, t)))
+            return
         k = rel[(rank, d)]
         before("G", [in_], [])
         if k is None:
@@ -304,16 +333,17 @@ def rank_program(g, core, T, topo):
 
     iota(("IOT", 0, WX), [[1, WX]])
     pick(("EXP", 0, 2048 - V16), ("ONE", 0, 2048 - V16), [[-1, 128 - VL], [0, 16]], -VL)
+    pick(("REB", 0, 128), ("ONE", 0, 128), [[0, 8], [-1, 16]], 0)
     pick(("PRB", 0, 1024), ("ONE", 0, 1024), [[-16, 8], [0, 8], [-1, 16]], 0)
     iota(("TMF", 0, 256), [[0, 16], [1, 16]])
     iota(("TRS", 0, 32), [[16, 32]], TRASH)
-    iota(("TRQ", 0, 16), [[16, 16]], 1024)
-    for b, lo, hi in (("EIN", 0, S), ("EIN", NULL, WX), ("GST", 0, S), ("GST", NULL, WX), ("EQ", 0, 4096), ("REQ", 0, 1280)):
+    for b, lo, hi in (("GST", 0, S), ("GST", NULL, WX), ("EQ", 0, 4096)):
         iota((b, lo, hi), [[0, hi - lo]])
     ts(KB, QF, 1.0, OP.add, -4096.0, OP.mult)
     ts(("MSK", 0, 1024), ("MSK", 0, 1024), 0.5, OP.is_gt)
     cp(("NBF", 0, S), ("NBI", 0, S))
     act(("NBF", S, WX), ("IOT", S, WX))
+    act(("REP", 0, 128), ("REB", 0, 128))
     ts(("WZ", 8, 16), GG, I15, OP.mult)
     cp(SC, N15)
     ts(B1, N15, -255.0, OP.mult, -1.0, OP.add)
@@ -344,13 +374,12 @@ def rank_program(g, core, T, topo):
     def later_consts():
         ts(("DQ", 0, 256), ("TMF", 0, 256), QF, OP.is_equal)
         ts(("TRS", 0, 32), ("TRS", 0, 32), QF, OP.add)
-        ts(("TRQ", 0, 16), ("TRQ", 0, 16), QF, OP.add)
         cp(TMPC, ("WTI", 0, 1))
         ts(("WZ", 0, 8), GG, TMPC, OP.mult, N15, OP.mult)
-        for e in (1, 2, 3):
-            lo = S + (e - 1) * GH
-            ts(col(27 + e), QF, float(e - 1), OP.is_equal)
-            act(("EIN", lo, lo + GH), ("IOT", lo, lo + GH), AF.Identity, scale=0.0, bias=col(27 + e))
+        for e, lo, hi in ((1, S, S + GH), (2, S + GH, S + 2 * GH), (3, S + 2 * GH, NULL), (4, 0, S), (4, NULL, WX)):
+            if lo != NULL:
+                ts(col(27 + e), QF, float(e - 1), OP.is_equal)
+            act(("EIN", lo, hi), ("IOT", lo, hi), AF.Identity, scale=0.0, bias=col(27 + e))
         for e in (2, 1, 3):
             lo = S + (e - 1) * GH
             cp(("SLU", (e - 1) * 24, e * 24), ("SNL", (e - 1) * 24, e * 24))
@@ -364,10 +393,6 @@ def rank_program(g, core, T, topo):
     def OLD(x, a, b):
         return ("OL", 2 * O8[x] + a, 2 * O8[x] + b)
 
-    def start_b(t):
-        cp(OLD("B", 0, 8), ("WAN", t * 10 + 2, t * 10 + 10))
-        cp(OFX("B", 0, 8), OLD("B", 0, 8))
-
     def start_a(t):
         cp(OLD("A", 6, 8), ("WAN", t * 10, t * 10 + 2))
         if t == 0:
@@ -379,7 +404,6 @@ def rank_program(g, core, T, topo):
     def own_v(x, win):
         cp(("ON" + x, 0, 128), ("I", NBW, OFX(x, 0, 8)))
         cp(("ZS" + x, 0, V16, 16), ("I", win, OFX(x, 0, VL // 16)))
-        scan(("SB" + x, 0, V16), ("MSK", 0, V16), ("ZS" + x, 0, V16), OP.mult, OP.add)
 
     def own_s(x, win):
         act(("SZ" + x, VL, 128), ("I", win, OFX(x, VL // 16, 8)))
@@ -388,12 +412,26 @@ def rank_program(g, core, T, topo):
         mm(("P" + x, 0, 384), ("SZ" + x, 0, 128), ("RS", 0, 384), True, False)
         mm(("P" + x, 256, 384), ("BS" + x, 0, 128), ("IDF", 0, 128), False, False)
 
+    def prep_b(t):
+        cp(OLD("B", 0, 8), ("WAN", t * 10 + 2, t * 10 + 10))
+        cp(OFX("B", 0, 8), OLD("B", 0, 8))
+        own_s("B", OWN)
+        own_v("B", OWN)
+
+    def ghosts_in(t):
+        for e in (2, 1, 3):
+            lo = (e - 1) * GH
+            act(("XT", S + lo, S + lo + GH), ("LG", t * 1152 + lo, t * 1152 + lo + GH))
+
     def own_t(x):
         act(("ST" + x, 0, 128), ("PT" + x, 128, 256))
 
-    def big_s(x, k):
-        a, pc = V16 + 512 * k, ("PC%d" % k, 0, 512)
+    def gather_s(x, k):
+        a = V16 + 512 * k
         act(("D" + x, a, a + 512), ("I", WIN, ("ON" + x, a // 16, a // 16 + 32)))
+
+    def diff(x, k):
+        a, pc = V16 + 512 * k, ("PC%d" % k, 0, 512)
         mm(pc, ("IDB", 0, 128), ("D" + x, a, a + 512), True, False)
         mm(pc, ("ST" + x, 0, 128), ("EXP", 512 * k, 512 * k + 512), False, True)
 
@@ -401,13 +439,24 @@ def rank_program(g, core, T, topo):
         a = V16 + 512 * k
         act(("N" + x, a, a + 512), ("PC%d" % k, 0, 512), AF.Relu, scale=-1.0)
 
+    def big_v(x):
+        scan(("SB" + x, 0, V16), ("MSK", 0, V16), ("ZS" + x, 0, V16), OP.mult, OP.add)
+        for k in range(4):
+            a, b = V16 // 4 * k, V16 // 4 * (k + 1)
+            tt(("D" + x, a, b), ("I", WIN, ("ON" + x, a // 16, b // 16)), ("SB" + x, a, b), OP.subtract)
+        for k in range(4):
+            a, b = V16 // 4 * k, V16 // 4 * (k + 1)
+            ts(("N" + x, a, b), ("D" + x, a, b), -1.0, OP.mult, 0.0, OP.max)
+
     def sums(ps, buf, rhs, lo, stop):
         for i in range(16):
             mm((ps, lo + i, lo + 256, 16), (buf, i, 2048, 16), (rhs, 0, 16), False, stop and i == 15)
 
+    def best_s(x):
+        act(("TA" + x, 0, 128), ("P" + x, 0, 128))
+
     def best(x):
         ps, m = "P" + x, "M" + x
-        cp(("TA" + x, 0, 128), (ps, 0, 128))
         tt((m, 0, 128), ("TA" + x, 0, 128), (ps, 128, 256), OP.min)
         tt((m, 128, 256), (m, 0, 128), (ps, 256, 384), OP.min)
         scan(("R" + x, 0, 128), ("MSK", 0, 128), (m, 128, 256), OP.mult, OP.max)
@@ -417,9 +466,12 @@ def rank_program(g, core, T, topo):
             mm((ps, c * w, c * w + w), (mat, c * 128, c * 128 + 128), rhs, True, True)
 
     def perm(x):
-        turn("PT" + x, 8, "PRF", ("R" + x, 15, 128, 16))
+        for c in range(8):
+            mm(("PT" + x, 64 + c * 8, 72 + c * 8, 1, 16), ("IDF", c * 16, c * 16 + 16), ("R" + x, 15, 128, 16), True, True)
 
     def step(x):
+        cp(("KQ" + x, 0, 64, 1, 16), ("PT" + x, 64, 128, 1, 16))
+        mm(("PT" + x, 0, 64), ("REP", 0, 128, 1, 16), ("KQ" + x, 0, 64, 1, 16), True, True)
         cp(("KS" + x, 0, 64), ("PT" + x, 0, 64))
         tt(("KI" + x, 0, 16), ("I", ("KS" + x, 0, 64), ("DG", 0, 1)), OLD(x, 0, 16), OP.max)
         ts(OLD(x, 0, 16), ("KI" + x, 0, 16), 4095, OP.bitwise_and)
@@ -455,18 +507,19 @@ def rank_program(g, core, T, topo):
         cp(("DBC", 0, 256), ("I", ("IOT", 0, WX), ("DOF", 0, 16)))
 
     def places3():
+        cp(("POI", 0, 16), ("SD", 0, 16))
         for c in range(16):
             ts(("EQ", c * 272, c * 256 + 256), ("DBC", 16 * c, 256), ("SD", c, c + 1), OP.is_equal)
+            if c == 5:
+                ts(("POI", 16, 32), ("POI", 0, 16), 511, OP.bitwise_and)
+            if c == 10:
+                cp(("POF", 0, 16), ("POI", 16, 32))
 
     def places4():
-        cp(("POI", 0, 16), ("SD", 0, 16))
-        ts(("POI", 16, 32), ("POI", 0, 16), 511, OP.bitwise_and)
-        cp(("POF", 0, 16), ("POI", 16, 32))
         for o, x in ((0, "A"), (128, "B")):
             p, q = o // 16, (o + VL) // 16
             tt(("TV", o, o + VL), ("I", ("PUL", 0, 512), ("POF", p, q)), ("ZS" + x, 0, V16, 16), OP.add)
             tt(("TV", o + VL, o + 128), ("I", ("PUL", 0, 512), ("POF", q, p + 8)), ("SZ" + x, VL, 128), OP.add)
-        ts(("TV2", 0, 256), ("TV", 0, 256), -0.5, OP.add, 16777216.0, OP.add)
 
     def places_s():
         act(("XD", 0, 256), ("I", WIN, ("DOF", 0, 16)))
@@ -480,6 +533,7 @@ def rank_program(g, core, T, topo):
         for k, x in ((0, "A"), (8, "B"), (16, "A")):
             ts(("STL", k, k + 8), ("R" + x, 15, 128, 16), 0.0, OP.is_equal)
         turn("PM2", 24, "PRB", ("STL", 0, 24))
+        places4()
         ts(("THE", 0, 16), ("PM", 32, 48), 0.0, OP.is_lt, THR, OP.mult)
         tt(("THE", 16, 32), ("THE", 0, 16), ("STL", 0, 16), OP.mult)
         tt(("RW", 0, 192), ("PM2", 0, 192), ("WM", 0, 192), OP.mult)
@@ -488,7 +542,7 @@ def rank_program(g, core, T, topo):
         for c in range(16):
             o = (c % 8) * 24 + (8 if c >= 8 else 16)
             mm(("PM", 8, 16), ("EQ", c * 256 + 128, c * 256 + 256), ("RW", o, o + 8), c == 0, c == 15)
-        places4()
+        ts(("TV2", 0, 256), ("TV", 0, 256), -0.5, OP.add, 16777216.0, OP.add)
         act(("VAL", 0, 256), ("TV2", 0, 256), AF.Identity, scale=HLF, bias=NVB[t])
         tt(("LB", 0, 16), ("PM", 0, 16), ("THE", 16, 32), OP.is_ge)
         turn("PM2", 16, "PRB", ("LB", 0, 16))
@@ -500,25 +554,19 @@ def rank_program(g, core, T, topo):
 
     def requests(t):
         act(("GV", 0, 256), ("I", ("GST", 0, WX), ("OFX", 0, 16)))
+        for e in (1, 2, 3):
+            act(("REQ", 512 * e + 1, 512 * e + 33), ("IOT", 0, CAP), AF.Identity, scale=0.0, bias=float(NULL))
         cp(("IND", 0, 256), ("I", ("EIN", 0, WX), ("OFX", 0, 16)))
         scan(("CNT", 0, 256), ("ONE", 0, 256), ("IND", 0, 256), OP.mult, OP.add)
         tt(("QC", 0, 256), ("IND", 0, 256), ("CNT", 0, 256), OP.mult)
         mm(("PC0", 0, 256), ("GM2", 0, 128), ("IND", 0, 256), True, False)
         mm(("PC0", 0, 256), GM, ("QC", 0, 256), False, True)
-        fill(("REQ", 32, 128), float(NULL))
         tt(("QX", 0, 256), ("PC0", 0, 256), ("DQ", 0, 256), OP.mult)
         scan(("QX", 256, 512), ("MSK", 0, 256), ("QX", 0, 256), OP.mult, OP.add)
-        r = [("RI", 16 * i, 16 * i + 16) for i in range(6)]
-        ts(r[0], ("QX", 271, 512, 16), -1.0, OP.add)
-        ts(r[1], r[0], 511, OP.bitwise_and)
-        ts(r[2], r[0], 4, OP.arith_shift_right, 96, OP.bitwise_and)
-        ts(("RF", 0, 16), r[1], float(CAP), OP.is_ge)
-        tt(r[3], r[1], r[2], OP.add)
-        tt(("RF", 16, 32), ("RF", 0, 16), ("TRQ", 0, 16), OP.mult)
-        tt(r[4], r[3], ("RF", 16, 32), OP.max)
-        cp(("RQF", 0, 16), r[4])
-        cp(("I", ("REQ", 0, 1280), ("RQF", 0, 16)), ("GV", 0, 256))
-        tt(("RX", 0, 96), ("REQ", 32, 128), ("DQ", 0, 96), OP.mult)
+        cp(("RQF", 0, 16), ("QX", 271, 512, 16))
+        cp(("I", ("REQ", 0, 2320), ("RQF", 0, 16)), ("GV", 0, 256))
+        for e in (1, 2, 3):
+            tt(("RX", 32 * e - 32, 32 * e), ("REQ", 512 * e + 1, 512 * e + 33), ("DQ", 0, CAP), OP.mult)
         scan(("RX", 96, 192), ("MSK", 0, 96), ("RX", 0, 96), OP.mult, OP.add)
         o = (t + 1) * 8
         cp(("RQO", o, o + 6), ("RX", 111, 192, 16))
@@ -527,58 +575,49 @@ def rank_program(g, core, T, topo):
             lands(("RIN", o + 2 * (e - 1), o + 2 * e), "rq%d_%d" % (e, t + 1), due((rank + e) % n))
 
     order = [("B", 0), ("A", 0), ("B", 1), ("A", 1), ("B", 2), ("A", 2)]
+    prep_b(0)
     for t in range(RO):
-        start_b(t)
-        own_s("B", OWN)
-        own_t("B")
-        own_v("B", OWN)
-        for e in (2, 1, 3):
-            lo = (e - 1) * GH
-            act(("XT", S + lo, S + lo + GH), ("LG", t * 1152 + lo, t * 1152 + lo + GH))
+        ghosts_in(t)
         for i, (x, h) in enumerate(order):
             y = "B" if x == "A" else "A"
-            last = i == 5
-            big_s(x, 0)
-            if i:
-                best(y)
-                if not last:
-                    perm(y)
-            if last:
+            big = rec(big_v, x)
+            if i == 5:
                 places_p()
-            big_s(x, 1)
-            if last:
-                places(t)
-            big = ("D" + x, 0, V16)
-            tt(big, ("I", WIN, ("ON" + x, 0, VL)), ("SB" + x, 0, V16), OP.subtract)
-            if i and not last:
-                step(y)
-            if i == 0:
-                start_a(t)
-            if last:
-                places2()
+            gather_s(x, 0)
+            own_t(x)
+            diff(x, 0)
+            if i == 5:
+                gather_s(x, 1)
+                diff(x, 1)
+                weave(big, rec(places, t), "ab" * 9)
+            else:
+                weave(big[:3], rec(best, y) if i else [], "ababab")
+                if i:
+                    perm(y)
+                gather_s(x, 1)
+                diff(x, 1)
+                weave(big[3:], rec(step, y) if i else rec(start_a, t), "abaabababab" if i else "aaaaaa")
             relu(x, 0)
-            sums("P" + x, "D" + x, "RD", 128, False)
-            if not last:
-                own_s(y, WIN)
             relu(x, 1)
-            ts(("N" + x, 0, V16), big, -1.0, OP.mult, 0.0, OP.max)
+            sums("P" + x, "D" + x, "RD", 128, False)
             sums("P" + x, "N" + x, "RN", 0, True)
-            if not last:
-                own_t(y)
+            if i < 5:
+                own_s(y, WIN)
+                best_s(x)
                 own_v(y, WIN)
             if t == 0 and i == 3:
                 later_consts()
-        places3()
+        weave(rec(best, "B"), rec(places2), "abab")
+        best_s("A")
         places_s()
-        best("A")
+        weave(rec(best, "A"), rec(places3), "bbbbbbabbbabbbabbbba")
         moves(t)
         if t + 1 < RO:
             ghosts(t + 1)
             perm("B")
             perm("A")
-            step("B")
-            step("A")
-            requests(t)
+            weave(rec(step, "B"), rec(step, "A"), "ab" * 5)
+            weave(rec(requests, t), rec(prep_b, t + 1), "aabababaabaaaaaa")
 
     for k, (a, b) in enumerate(part):
         ts(("DB", a, b), ("XT", a, b), 0.0, OP.is_lt)

from concourse.mybir import AluOpType, ActivationFunctionType

S, GH, CAP, RO = 1792, 384, 32, 4
NULL, WX, TRASH = 2944, 2960, 3072
VL = 64
V16 = 16 * VL
OP = AluOpType
AF = ActivationFunctionType
SIZES = {
    "bfloat16": "XT 3584,EIN 2960,PUL 512,ZSA 2048,ZSB 2048,MSK 1024,SBA 1024,SBB 1024,DA 2048,DB 2048,NA 2048,NB 2048,EXP 1024,"
                "ONE 1024,EQ 4096,PRB 1024,IDB 128,IDN 128,EMP 128,EMN 128,GM 128,GM2 128,RD 16,RN 16,RS 384,WZ 16,DQ 256,SZA 128,"
                "SZB 128,STA 128,STB 128,XD 256,VAL 512,STL 24,RW 192,LB 16,IND 256,CNT 256,QC 256,GS 4608,LG 4608,RG 1536,YO 1792,"
                "REB 128",
    "float32": "NBF 2960,IOT 2960,GST 2960,REQ 2320,PRF 1024,IDF 128,WM 192,COL 64,GG 64,TMF 256,TM2 512,TRS 32,BSA 128,"
               "BSB 128,TAA 128,TAB 128,MA 256,MB 256,RA 128,RB 128,KSA 64,KSB 64,DL 32,KD 128,SD 32,INV 16,TV 256,TV2 256,THE 32,"
               "KL 128,LW 64,QX 512,GV 256,RX 192,REP 128,KQA 64,KQB 64",
    "int32": "NBI 1792,WTI 8,WAN 40,SND 72,SNL 72,CI 32,OL 32,KIA 16,KIB 16,ZI 128,POI 32,RSN 24",
    "uint16": "SNU 72,SLU 72,DG 8,OFX 16,ONA 128,ONB 128,DOF 16,POF 16,DBC 256,OFS 32,RQF 16,RQO 32,RIN 32,RRQ 32",
}
SCRATCH = {}
for _d, _l in SIZES.items():
    for _x in _l.split(","):
        SCRATCH[_x.split()[0]] = ("sbuf", [128, int(_x.split()[1])], _d)
BANKS = ("PA", "PB", "PC0", "PC1", "PTA", "PTB", "PM", "PM2")
for _x in BANKS:
    SCRATCH[_x] = ("psum", [128, 512], "float32")
SEMAPHORES = (["sV", "sS", "sP", "sG", "ls", "rs"] + ["ld%d" % i for i in range(8)] + ["st%d" % i for i in range(4)]
              + ["ga%d_%d" % (e, t) for e in (1, 2, 3) for t in range(4)] + ["rq%d_%d" % (e, t) for e in (1, 2, 3) for t in (1, 2, 3)]
              + ["sn%d" % e for e in (1, 2, 3)] + ["rg%d" % t for t in range(4)] + ["rr%d" % t for t in (1, 2, 3)])


def routes(T, topo):
    n = len(T.cores)
    rel = {}
    for r in range(n):
        c = T.cores[r]
        near = True
        for e in range(1, n):
            d = (r + e) % n
            if topo.may_write(c, T.cores[d]):
                rel[(r, d)] = None
                continue
            cand = [k for k in topo.cores_of(c) if k != c and topo.may_write(k, T.cores[d]) and topo.may_write(c, k)]
            pick = [k for k in cand if (topo.die(k) == topo.die(c)) == near] or cand
            rel[(r, d)] = pick[0]
            near = False
    return rel


def count(m):
    return bin(m).count("1")


def relay_program(g, core, T, topo, r, d):
    n = len(T.cores)
    src, dst = T.cores[r], T.cores[d]
    e, eq = (d - r) % n, (r - d) % n
    k_in, m = count(topo.mask(src, core)), topo.mask(core, dst)
    rid, pid = topo.addr(dst, core)

    def on(sem, out, in_, rsem):
        g.wait_ge(T.sem[sem], k_in)
        g.remote_dma(out, in_, T.sem[rsem], T.sem["ls"], pid, rid, m)
    for t in range(RO):
        on("rg%d" % t, T["LG"][:, t * 1152 + (e - 1) * GH:t * 1152 + e * GH], T["RG"][:, t * GH:(t + 1) * GH], "ga%d_%d" % (e, t))
        if t == 0:
            on("rs", T["SNL"][:, (e - 1) * 24:e * 24], T["RSN"][:, 0:24], "sn%d" % e)
        else:
            on("rr%d" % t, T["RIN"][:, t * 8 + 2 * (eq - 1):t * 8 + 2 * eq], T["RRQ"][:, t * 8:t * 8 + 2], "rq%d_%d" % (eq, t))
    g.wait_ge(T.sem["ls"], 2 * RO * count(m))


def rank_program(g, core, T, topo):
    rel = routes(T, topo)
    rank = T.rank_of(core)
    if rank is None:
        for (r, d), k in rel.items():
            if k == core:
                relay_program(g, core, T, topo, r, d)
        return
    n = len(T.cores)
    queue = {"V": g.vector, "S": g.scalar, "P": g.tensor, "G": g, "Y": g.sync}
    clock = {k: {} for k in queue}
    total = {}
    acc = {}
    tape = [None]

    def need(q, ev, ck):
        s, v = ev
        if clock[q].get(s, 0) < v:
            queue[q].wait_ge(T.sem[s], v)
            clock[q][s] = v
        for a, b in ck.items():
            if clock[q].get(a, 0) < b:
                clock[q][a] = b

    def span(s):
        return (s[0], 0, 512) if s[0] in BANKS else (s[0], s[1], s[2])

    def before(q, reads, writes):
        todo = []
        for w, lst in ((False, reads), (True, writes)):
            for s in lst:
                b, lo, hi = span(s)
                for a in acc.get(b, []):
                    if a[0] < hi and lo < a[1]:
                        if not w and not a[2] and not (b in BANKS and a[3] != q):
                            continue
                        if a[3] == q and (w or b in BANKS and q == "P"):
                            continue
                        todo.append((a[4], a[5]))
        todo.sort(key=lambda x: -x[0][1])
        for ev, ck in todo:
            if clock[q].get(ev[0], 0) < ev[1]:
                need(q, ev, ck)

    def after(q, ev, reads, writes, by):
        ck = dict(clock[by])
        for w, lst in ((False, reads), (True, writes)):
            for s in lst:
                b, lo, hi = span(s)
                old = acc.setdefault(b, [])
                if w and len(s) < 4:
                    old[:] = [a for a in old if not (lo <= a[0] and a[1] <= hi)]
                elif not w:
                    old[:] = [a for a in old if a[2] or a[3] != q or not (lo <= a[0] and a[1] <= hi)]
                old.append([lo, hi, w, q, ev, ck])

    def do(q, fn, reads, writes):
        if tape[0] is not None:
            tape[0].append((q, fn, reads, writes))
            return
        before(q, reads, writes)
        s = "s" + q
        total[s] = total.get(s, 0) + 1
        fn(queue[q]).then_inc(T.sem[s], 1)
        after(q, (s, total[s]), reads, writes, q)

    def rec(f, *args):
        tape[0] = []
        f(*args)
        out, tape[0] = tape[0], None
        return out

    def weave(a, b, pat):
        lists = {"a": a[:], "b": b[:]}
        for c in pat + "a" * len(a) + "b" * len(b):
            lst = lists[c]
            seen = False
            while lst and not (seen and lst[0][0] == "V"):
                seen = seen or lst[0][0] == "V"
                x = lst.pop(0)
                if x[0] == "send":
                    send(*x[1])
                else:
                    do(*x)

    def dma(q, sem, out, in_, reads, writes):
        before(q, reads, writes)
        total[sem] = total.get(sem, 0) + 16
        queue[q].dma_start(out, in_).then_inc(T.sem[sem], 16)
        after(sem, (sem, total[sem]), reads, writes, q)

    def lands(s, sem, k):
        total[sem] = total.get(sem, 0) + k
        acc.setdefault(s[0], []).append([s[1], s[2], True, "remote", (sem, total[sem]), {}])

    def ap(s):
        if s[0] == "I":
            return ap(s[1]).indirect(ap(s[2]))
        if len(s) == 5:
            return T[s[0]][0:s[4], s[1]:s[2]]
        return T[s[0]][:, s[1]:s[2]] if len(s) == 3 else T[s[0]][:, s[1]:s[2]:s[3]]

    def rd(*ss):
        out = []
        for s in ss:
            if isinstance(s, tuple):
                out += [s[1], s[2]] if s[0] == "I" else [s]
        return out

    def wr(s):
        return [s[1]] if s[0] == "I" else [s]

    def val(s):
        return ap(s) if isinstance(s, tuple) else s

    def tt(out, a, b, op):
        do("V", lambda v: v.tensor_tensor(ap(out), ap(a), ap(b), op), rd(a, b), wr(out))

    def ts(out, a, s1, op0, s2=None, op1=None):
        if op1 is None:
            do("V", lambda v: v.tensor_scalar(ap(out), ap(a), val(s1), None, op0), rd(a, s1), wr(out))
        else:
            do("V", lambda v: v.tensor_scalar(ap(out), ap(a), val(s1), val(s2), op0, op1), rd(a, s1, s2), wr(out))

    def cp(out, a):
        do("V", lambda v: v.tensor_copy(ap(out), ap(a)), rd(a) + (rd(out)[1:] if out[0] == "I" else []), wr(out))

    def scan(out, d0, d1, op0, op1):
        do("V", lambda v: v.tensor_tensor_scan(ap(out), ap(d0), ap(d1), 0.0, op0, op1), rd(d0, d1), wr(out))

    def fill(out, c):
        do("V", lambda v: v.memset(ap(out), c), [], wr(out))

    def act(out, a, func=AF.Copy, **kw):
        do("S", lambda s: s.activation(ap(out), ap(a), func, **{k: val(x) for k, x in kw.items()}), rd(a, *kw.values()), wr(out))

    def mm(out, l, r, start, stop):
        do("P", lambda p: p.matmul(ap(out), ap(l), ap(r), start, stop), rd(l, r), wr(out))

    def iota(out, pat, base=0, cm=0):
        kw = {} if SCRATCH[out[0]][2] == "int32" else {"allow_small_or_imprecise_dtypes": True}
        do("G", lambda q: q.iota(ap(out), pat, base, cm, **kw), [], wr(out))

    def pick(out, a, pat, base):
        do("G", lambda q: q.affine_select(ap(out), ap(a), pat, OP.is_equal, 0.0, base, 1), rd(a), wr(out))

    def send(in_, d, kind, e, t):
        if tape[0] is not None:
            tape[0].append(("send", (in_, d, kind, e, t)))
            return
        k = rel[(rank, d)]
        before("G", [in_], [])
        if k is None:
            out, sem = {"g": (("LG", t * 1152 + (e - 1) * GH), "ga%d_%d" % (e, t)), "s": (("SNL", (e - 1) * 24), "sn%d" % e),
                        "q": (("RIN", t * 8 + 2 * (e - 1)), "rq%d_%d" % (e, t))}[kind]
        else:
            out, sem = {"g": (("RG", t * GH), "rg%d" % t), "s": (("RSN", 0), "rs"), "q": (("RRQ", t * 8), "rr%d" % t)}[kind]
        to = T.cores[d] if k is None else k
        rid, pid = topo.addr(to, core)
        m = topo.mask(core, to)
        g.remote_dma(T[out[0]][:, out[1]:out[1] + in_[2] - in_[1]], ap(in_), T.sem[sem], T.sem["ls"], pid, rid, m)
        total["ls"] = total.get("ls", 0) + count(m)

    def due(d):
        k = rel[(d, rank)]
        return count(topo.mask(T.cores[d] if k is None else k, core))

    def col(i):
        return ("COL", i, i + 1)

    def ci(i):
        return ("CI", i, i + 1)

    QF, GF, N15, I15, SC, B1, HLF, THR, QP, TMPC, KB = [col(i) for i in range(11)]
    NVB = [col(12 + i) for i in range(4)]
    WIN, OWN, NBW = ("XT", 0, WX), ("XT", 0, S), ("NBF", 0, WX)
    GM, GG = ("GM", 0, 128), ("GG", 0, 8)

    dma("Y", "ld0", T["XT"][:, 0:S], T.x0[:, :], [], [OWN])
    dma("S", "ld1", T["SND"][:, :], T.snd[:, :], [], [("SND", 0, 72)])
    dma("Y", "ld2", T["NBI"][:, :], T.nb[:, :], [], [("NBI", 0, S)])
    dma("S", "ld3", T["WAN"][:, :], T.wants[:, :], [], [("WAN", 0, 40)])
    dma("S", "ld4", T["WTI"][:, 0:1], T.wt[:, :], [], [("WTI", 0, 1)])
    dma("S", "ld5", T["PUL"][:, :], T.pull[:, :], [], [("PUL", 0, 512)])

    iota(ci(0), [[1, 1]], 0, 1)
    iota(("TMF", 0, 128), [[1, 8], [0, 16]])
    iota(("TM2", 0, 128), [[0, 8], [1, 16]])
    iota(GG, [[1, 8]])
    iota(("QX", 0, 256), [[1, 16], [0, 16]])
    iota(("MSK", 0, 1024), [[0, 64], [1, 16]])
    fill(("ONE", 0, 1024), 1.0)
    pick(("IDB", 0, 128), ("ONE", 0, 128), [[-1, 128]], 0)
    fill(("XT", NULL, WX), 0.0)
    ts(ci(1), ci(0), 15, OP.bitwise_and)
    ts(ci(2), ci(0), 4, OP.logical_shift_right)
    cp(QF, ci(1))
    cp(GF, ci(2))
    ts(N15, QF, 15.0, OP.is_lt)
    ts(I15, QF, 15.0, OP.is_equal)
    ts(TMPC, I15, -256.0, OP.mult)
    ts(GM, ("TMF", 0, 128), GF, OP.is_equal)
    ts(("TM2", 0, 128), ("TM2", 0, 128), 15.0, OP.is_lt)
    tt(("TM2", 0, 128), ("TM2", 0, 128), GM, OP.mult)
    ts(("EMP", 0, 128), ("TM2", 0, 128), TMPC, OP.mult)
    ts(("EMN", 0, 128), ("EMP", 0, 128), -1.0, OP.mult)
    cp(("SNU", 0, 72), ("SND", 0, 72))
    for x in "AB":
        for k in (0, 1024):
            act(("ZS" + x, k, k + 1024), ("ONE", 0, 1024), AF.Identity, scale=0.0)
        act(("SZ" + x, 0, 128), ("ONE", 0, 128), AF.Identity, scale=0.0)
    fill(("OL", 0, 32), 0)
    ts(GG, GG, GF, OP.is_equal)
    ts(("RD", 0, 8), GG, N15, OP.mult, 16777216.0, OP.mult)
    ts(("RD", 8, 16), GG, I15, OP.mult, 69632.0, OP.mult)
    cp(("RN", 0, 8), ("RD", 0, 8))
    cp(("RN", 8, 16), ("RD", 0, 8))
    ts(col(16), N15, -16777216.0, OP.mult)
    ts(col(17), I15, -69632.0, OP.mult)
    ts(col(18), GF, 8.0, OP.add)
    ts(("TM2", 0, 256), ("QX", 0, 256), GF, OP.is_equal, col(16), OP.mult)
    ts(("TM2", 256, 512), ("QX", 0, 256), col(18), OP.is_equal, col(17), OP.mult)
    fill(("RS", 0, 128), 0.0)
    tt(("RS", 128, 384), ("TM2", 0, 256), ("TM2", 256, 512), OP.add)
    cp(("IDF", 0, 128), ("IDB", 0, 128))
    ts(("IDN", 0, 128), ("IDB", 0, 128), -1.0, OP.mult)
    ts(ci(3), ci(1), 7, OP.bitwise_and)
    ts(ci(4), ci(1), 3, OP.logical_shift_right)
    ts(col(19), ci(3), 8.0, OP.mult)
    ts(col(20), ci(4), 8.0, OP.mult)
    tt(col(21), col(19), GF, OP.add)
    tt(col(22), col(21), col(19), OP.add)
    tt(col(23), col(22), col(20), OP.add)
    cp(("DG", 0, 1), col(21))
    cp(("DG", 2, 3), col(23))
    cp(("DG", 3, 4), col(23))
    ban = ["PC0", "PC1", "PTA", "PTB"]
    part = [(448 * k, 448 * (k + 1)) for k in range(4)]
    for k, (a, b) in enumerate(part):
        ts(("YO", a, b), ("XT", a, b), 0.0, OP.is_lt)
        mm((ban[k], 0, 448), ("EMP", 0, 128), ("YO", a, b), True, True)
    for k, (a, b) in enumerate(part):
        tt(("XT", a, b), ("XT", a, b), (ban[k], 0, 448), OP.add)

    def ghosts(t):
        at = t * 1152
        act(("GS", at, at + 384), ("I", OWN, ("SNU", 0, 24)))
        cp(("GS", at + 768, at + 1152), ("I", OWN, ("SNU", 48, 72)))
        send(("GS", at, at + 384), (rank + 1) % n, "g", 1, t)
        send(("GS", at + 768, at + 1152), (rank + 3) % n, "g", 3, t)
        act(("GS", at + 384, at + 576), ("I", OWN, ("SNU", 24, 36)))
        cp(("GS", at + 576, at + 768), ("I", OWN, ("SNU", 36, 48)))
        send(("GS", at + 384, at + 768), (rank + 2) % n, "g", 2, t)
        for e in (1, 2, 3):
            lands(("LG", at + (e - 1) * GH, at + e * GH), "ga%d_%d" % (e, t), due((rank - e) % n))

    ghosts(0)
    for e in (1, 3, 2):
        send(("SND", (e - 1) * 24, e * 24), (rank + e) % n, "s", e, 0)
        lands(("SNL", (e - 1) * 24, e * 24), "sn%d" % e, due((rank - e) % n))

    iota(("IOT", 0, WX), [[1, WX]])
    pick(("EXP", 0, 2048 - V16), ("ONE", 0, 2048 - V16), [[-1, 128 - VL], [0, 16]], -VL)
    pick(("REB", 0, 128), ("ONE", 0, 128), [[0, 8], [-1, 16]], 0)
    pick(("PRB", 0, 1024), ("ONE", 0, 1024), [[-16, 8], [0, 8], [-1, 16]], 0)
    iota(("TMF", 0, 256), [[0, 16], [1, 16]])
    iota(("TRS", 0, 32), [[16, 32]], TRASH)
    for b, lo, hi in (("GST", 0, S), ("GST", NULL, WX), ("EQ", 0, 4096)):
        iota((b, lo, hi), [[0, hi - lo]])
    ts(KB, QF, 1.0, OP.add, -4096.0, OP.mult)
    ts(("MSK", 0, 1024), ("MSK", 0, 1024), 0.5, OP.is_gt)
    cp(("NBF", 0, S), ("NBI", 0, S))
    act(("NBF", S, WX), ("IOT", S, WX))
    act(("REP", 0, 128), ("REB", 0, 128))
    ts(("WZ", 8, 16), GG, I15, OP.mult)
    cp(SC, N15)
    ts(B1, N15, -255.0, OP.mult, -1.0, OP.add)
    ts(HLF, N15, 0.5, OP.mult)
    ts(col(24), N15, -8388608.0, OP.mult)
    for t in range(RO):
        ts(NVB[t], I15, float(192 + t), OP.mult, col(24), OP.add)
    fill(QP, 32768.0)
    for k in range(4):
        ts(ci(8), ci(1), k, OP.logical_shift_right, 1, OP.bitwise_and)
        ts(col(25), ci(8), 2.0 ** -(2 ** k) - 1.0, OP.mult, 1.0, OP.add)
        tt(QP, QP, col(25), OP.mult)
    for c in range(8):
        w = 2.0 ** (17 * (7 - c) - 44)
        ts(("WM", c * 24, c * 24 + 8), GG, QP, OP.mult, w, OP.mult)
        ts(("WM", c * 24 + 8, c * 24 + 16), GG, QP, OP.mult, w, OP.mult)
        ts(("WM", c * 24 + 16, c * 24 + 24), GG, 2.0 ** 92, OP.mult)
        fill(("GG", 16 + c, 17 + c), 2.0 * w)
    tt(("GG", 32, 40), GG, ("GG", 16, 24), OP.mult)
    tt(("GG", 32, 36), ("GG", 32, 36), ("GG", 36, 40), OP.add)
    tt(("GG", 32, 34), ("GG", 32, 34), ("GG", 34, 36), OP.add)
    tt(col(26), ("GG", 32, 33), ("GG", 33, 34), OP.add)
    tt(THR, col(26), QP, OP.mult)
    ts(col(27), QF, 1.0, OP.add, 512.0, OP.mult)
    ts(("GM2", 0, 128), GM, col(27), OP.mult)
    act(("PRF", 0, 1024), ("PRB", 0, 1024))

    def later_consts():
        ts(("DQ", 0, 256), ("TMF", 0, 256), QF, OP.is_equal)
        ts(("TRS", 0, 32), ("TRS", 0, 32), QF, OP.add)
        cp(TMPC, ("WTI", 0, 1))
        ts(("WZ", 0, 8), GG, TMPC, OP.mult, N15, OP.mult)
        for e, lo, hi in ((1, S, S + GH), (2, S + GH, S + 2 * GH), (3, S + 2 * GH, NULL), (4, 0, S), (4, NULL, WX)):
            if lo != NULL:
                ts(col(27 + e), QF, float(e - 1), OP.is_equal)
            act(("EIN", lo, hi), ("IOT", lo, hi), AF.Identity, scale=0.0, bias=col(27 + e))
        for e in (2, 1, 3):
            lo = S + (e - 1) * GH
            cp(("SLU", (e - 1) * 24, e * 24), ("SNL", (e - 1) * 24, e * 24))
            act(("GST", lo, lo + GH), ("I", ("IOT", 0, S), ("SLU", (e - 1) * 24, e * 24)))

    O8 = {"A": 0, "B": 8}

    def OFX(x, a, b):
        return ("OFX", O8[x] + a, O8[x] + b)

    def OLD(x, a, b):
        return ("OL", 2 * O8[x] + a, 2 * O8[x] + b)

    def start_a(t):
        cp(OLD("A", 6, 8), ("WAN", t * 10, t * 10 + 2))
        if t == 0:
            fill(OLD("A", 0, 6), NULL)
        else:
            cp(OLD("A", 0, 6), ("RIN", t * 8, t * 8 + 6))
        cp(OFX("A", 0, 8), OLD("A", 0, 8))

    def own_v(x, win):
        cp(("ON" + x, 0, 128), ("I", NBW, OFX(x, 0, 8)))
        cp(("ZS" + x, 0, V16, 16), ("I", win, OFX(x, 0, VL // 16)))

    def own_s(x, win):
        act(("SZ" + x, VL, 128), ("I", win, OFX(x, VL // 16, 8)))
        mm(("PT" + x, 128, 256), ("SZ" + x, 0, 128), ("IDN", 0, 128), True, True)
        act(("BS" + x, 0, 128), ("I", NBW, OFX(x, 0, 8)), AF.Identity, bias=KB)
        mm(("P" + x, 0, 384), ("SZ" + x, 0, 128), ("RS", 0, 384), True, False)
        mm(("P" + x, 256, 384), ("BS" + x, 0, 128), ("IDF", 0, 128), False, False)

    def prep_b(t):
        cp(OLD("B", 0, 8), ("WAN", t * 10 + 2, t * 10 + 10))
        cp(OFX("B", 0, 8), OLD("B", 0, 8))
        own_s("B", OWN)
        own_v("B", OWN)

    def ghosts_in(t):
        for e in (2, 1, 3):
            lo = (e - 1) * GH
            act(("XT", S + lo, S + lo + GH), ("LG", t * 1152 + lo, t * 1152 + lo + GH))

    def own_t(x):
        act(("ST" + x, 0, 128), ("PT" + x, 128, 256))

    def gather_s(x, k):
        a = V16 + 512 * k
        act(("D" + x, a, a + 512), ("I", WIN, ("ON" + x, a // 16, a // 16 + 32)))

    def diff(x, k):
        a, pc = V16 + 512 * k, ("PC%d" % k, 0, 512)
        mm(pc, ("IDB", 0, 128), ("D" + x, a, a + 512), True, False)
        mm(pc, ("ST" + x, 0, 128), ("EXP", 512 * k, 512 * k + 512), False, True)

    def relu(x, k):
        a = V16 + 512 * k
        act(("N" + x, a, a + 512), ("PC%d" % k, 0, 512), AF.Relu, scale=-1.0)

    def big_v(x):
        scan(("SB" + x, 0, V16), ("MSK", 0, V16), ("ZS" + x, 0, V16), OP.mult, OP.add)
        for k in range(4):
            a, b = V16 // 4 * k, V16 // 4 * (k + 1)
            tt(("D" + x, a, b), ("I", WIN, ("ON" + x, a // 16, b // 16)), ("SB" + x, a, b), OP.subtract)
        for k in range(4):
            a, b = V16 // 4 * k, V16 // 4 * (k + 1)
            ts(("N" + x, a, b), ("D" + x, a, b), -1.0, OP.mult, 0.0, OP.max)

    def sums(ps, buf, rhs, lo, stop):
        for i in range(16):
            mm((ps, lo + i, lo + 256, 16), (buf, i, 2048, 16), (rhs, 0, 16), False, stop and i == 15)

    def best_s(x):
        act(("TA" + x, 0, 128), ("P" + x, 0, 128))

    def best(x):
        ps, m = "P" + x, "M" + x
        tt((m, 0, 128), ("TA" + x, 0, 128), (ps, 128, 256), OP.min)
        tt((m, 128, 256), (m, 0, 128), (ps, 256, 384), OP.min)
        scan(("R" + x, 0, 128), ("MSK", 0, 128), (m, 128, 256), OP.mult, OP.max)

    def turn(ps, w, mat, rhs):
        for c in range(8):
            mm((ps, c * w, c * w + w), (mat, c * 128, c * 128 + 128), rhs, True, True)

    def perm(x):
        for c in range(8):
            mm(("PT" + x, 64 + c * 8, 72 + c * 8, 1, 16), ("IDF", c * 16, c * 16 + 16), ("R" + x, 15, 128, 16), True, True)

    def step(x):
        cp(("KQ" + x, 0, 64, 1, 16), ("PT" + x, 64, 128, 1, 16))
        mm(("PT" + x, 0, 64), ("REP", 0, 128, 1, 16), ("KQ" + x, 0, 64, 1, 16), True, True)
        cp(("KS" + x, 0, 64), ("PT" + x, 0, 64))
        tt(("KI" + x, 0, 16), ("I", ("KS" + x, 0, 64), ("DG", 0, 1)), OLD(x, 0, 16), OP.max)
        ts(OLD(x, 0, 16), ("KI" + x, 0, 16), 4095, OP.bitwise_and)
        cp(OFX(x, 0, 8), OLD(x, 0, 8))

    def places_p():
        for b, x in enumerate("AB"):
            for k in (0, 8):
                o = ("PM", 2 * k + 8 * b, 2 * k + 8 * b + 8)
                mm(o, ("ZS" + x, 0, 2048, 16), ("WZ", k, k + 8), True, False)
                mm(o, ("SZ" + x, 0, 128), ("WZ", k, k + 8), False, True)

    def places(t):
        z = [("ZI", 16 * i, 16 * i + 16) for i in range(8)]
        ts(("DL", 16, 32), ("PM", 16, 32), 0.0, OP.is_lt, float(NULL), OP.mult)
        cp(z[0], ("PM", 0, 16))
        ts(z[1], z[0], 2047, OP.bitwise_and)
        tt(z[2], z[1], z[1], OP.mult)
        ts(z[3], z[2], float(97 * t * 32), OP.add)
        ts(z[4], z[3], 5, OP.logical_shift_right, 2047, OP.bitwise_and)
        ts(z[5], z[4], float(S), OP.is_ge, -float(S), OP.mult)
        tt(z[6], z[4], z[5], OP.add)
        tt(("DL", 0, 16), z[6], ("DL", 16, 32), OP.max)
        turn("PM2", 16, "PRF", ("DL", 0, 16))
        for k, x in ((0, "A"), (8, "B")):
            ts(("INV", k, k + 8), OLD(x, 0, 8), float(S), OP.is_ge, float(NULL), OP.mult)
            cp(("SD", 16 + k, 24 + k), OLD(x, 0, 8))

    def places2():
        cp(("KD", 0, 128), ("PM2", 0, 128))
        tt(("SD", 0, 16), ("I", ("KD", 0, 128), ("DG", 2, 3)), ("INV", 0, 16), OP.max)
        cp(("DOF", 0, 16), ("SD", 0, 16))
        cp(("DBC", 0, 256), ("I", ("IOT", 0, WX), ("DOF", 0, 16)))

    def places3():
        cp(("POI", 0, 16), ("SD", 0, 16))
        for c in range(16):
            ts(("EQ", c * 272, c * 256 + 256), ("DBC", 16 * c, 256), ("SD", c, c + 1), OP.is_equal)
            if c == 5:
                ts(("POI", 16, 32), ("POI", 0, 16), 511, OP.bitwise_and)
            if c == 10:
                cp(("POF", 0, 16), ("POI", 16, 32))

    def places4():
        for o, x in ((0, "A"), (128, "B")):
            p, q = o // 16, (o + VL) // 16
            tt(("TV", o, o + VL), ("I", ("PUL", 0, 512), ("POF", p, q)), ("ZS" + x, 0, V16, 16), OP.add)
            tt(("TV", o + VL, o + 128), ("I", ("PUL", 0, 512), ("POF", q, p + 8)), ("SZ" + x, VL, 128), OP.add)

    def places_s():
        act(("XD", 0, 256), ("I", WIN, ("DOF", 0, 16)))
        for b in (0, 1):
            mm(("PM", 32 + 8 * b, 40 + 8 * b), ("XD", 128 * b, 128 * b + 128), ("WZ", 8, 16), True, True)
        for o, x in ((256, "A"), (384, "B")):
            act(("VAL", o, o + VL), ("ZS" + x, 0, V16, 16), AF.Identity, scale=SC, bias=B1)
            act(("VAL", o + VL, o + 128), ("SZ" + x, VL, 128), AF.Identity, scale=SC, bias=B1)

    def moves(t):
        for k, x in ((0, "A"), (8, "B"), (16, "A")):
            ts(("STL", k, k + 8), ("R" + x, 15, 128, 16), 0.0, OP.is_equal)
        turn("PM2", 24, "PRB", ("STL", 0, 24))
        places4()
        ts(("THE", 0, 16), ("PM", 32, 48), 0.0, OP.is_lt, THR, OP.mult)
        tt(("THE", 16, 32), ("THE", 0, 16), ("STL", 0, 16), OP.mult)
        tt(("RW", 0, 192), ("PM2", 0, 192), ("WM", 0, 192), OP.mult)
        for c in range(8):
            mm(("PM", 0, 8), ("EQ", c * 256, c * 256 + 128), ("RW", c * 24, c * 24 + 8), c == 0, c == 7)
        for c in range(16):
            o = (c % 8) * 24 + (8 if c >= 8 else 16)
            mm(("PM", 8, 16), ("EQ", c * 256 + 128, c * 256 + 256), ("RW", o, o + 8), c == 0, c == 15)
        ts(("TV2", 0, 256), ("TV", 0, 256), -0.5, OP.add, 16777216.0, OP.add)
        act(("VAL", 0, 256), ("TV2", 0, 256), AF.Identity, scale=HLF, bias=NVB[t])
        tt(("LB", 0, 16), ("PM", 0, 16), ("THE", 16, 32), OP.is_ge)
        turn("PM2", 16, "PRB", ("LB", 0, 16))
        cp(("KL", 0, 128), ("PM2", 0, 128))
        tt(("LW", 0, 32), ("I", ("KL", 0, 128), ("DG", 2, 4)), ("TRS", 0, 32), OP.mult)
        tt(("LW", 32, 64), ("LW", 0, 32), ("SD", 0, 32), OP.max)
        cp(("OFS", 0, 32), ("LW", 32, 64))
        cp(("I", ("XT", 0, 3584), ("OFS", 0, 32)), ("VAL", 0, 512))

    def requests(t):
        act(("GV", 0, 256), ("I", ("GST", 0, WX), ("OFX", 0, 16)))
        for e in (1, 2, 3):
            act(("REQ", 512 * e + 1, 512 * e + 33), ("IOT", 0, CAP), AF.Identity, scale=0.0, bias=float(NULL))
        cp(("IND", 0, 256), ("I", ("EIN", 0, WX), ("OFX", 0, 16)))
        scan(("CNT", 0, 256), ("ONE", 0, 256), ("IND", 0, 256), OP.mult, OP.add)
        tt(("QC", 0, 256), ("IND", 0, 256), ("CNT", 0, 256), OP.mult)
        mm(("PC0", 0, 256), ("GM2", 0, 128), ("IND", 0, 256), True, False)
        mm(("PC0", 0, 256), GM, ("QC", 0, 256), False, True)
        tt(("QX", 0, 256), ("PC0", 0, 256), ("DQ", 0, 256), OP.mult)
        scan(("QX", 256, 512), ("MSK", 0, 256), ("QX", 0, 256), OP.mult, OP.add)
        cp(("RQF", 0, 16), ("QX", 271, 512, 16))
        cp(("I", ("REQ", 0, 2320), ("RQF", 0, 16)), ("GV", 0, 256))
        for e in (1, 2, 3):
            tt(("RX", 32 * e - 32, 32 * e), ("REQ", 512 * e + 1, 512 * e + 33), ("DQ", 0, CAP), OP.mult)
        scan(("RX", 96, 192), ("MSK", 0, 96), ("RX", 0, 96), OP.mult, OP.add)
        o = (t + 1) * 8
        cp(("RQO", o, o + 6), ("RX", 111, 192, 16))
        for e in (1, 3, 2):
            send(("RQO", o + 2 * (e - 1), o + 2 * e), (rank - e) % n, "q", e, t + 1)
            lands(("RIN", o + 2 * (e - 1), o + 2 * e), "rq%d_%d" % (e, t + 1), due((rank + e) % n))

    order = [("B", 0), ("A", 0), ("B", 1), ("A", 1), ("B", 2), ("A", 2)]
    prep_b(0)
    for t in range(RO):
        ghosts_in(t)
        for i, (x, h) in enumerate(order):
            y = "B" if x == "A" else "A"
            big = rec(big_v, x)
            if i == 5:
                places_p()
            gather_s(x, 0)
            own_t(x)
            diff(x, 0)
            if i == 5:
                gather_s(x, 1)
                diff(x, 1)
                weave(big, rec(places, t), "ab" * 9)
            else:
                weave(big[:3], rec(best, y) if i else [], "ababab")
                if i:
                    perm(y)
                gather_s(x, 1)
                diff(x, 1)
                weave(big[3:], rec(step, y) if i else rec(start_a, t), "abaabababab" if i else "aaaaaa")
            relu(x, 0)
            relu(x, 1)
            sums("P" + x, "D" + x, "RD", 128, False)
            sums("P" + x, "N" + x, "RN", 0, True)
            if i < 5:
                own_s(y, WIN)
                best_s(x)
                own_v(y, WIN)
            if t == 0 and i == 3:
                later_consts()
        weave(rec(best, "B"), rec(places2), "abab")
        best_s("A")
        places_s()
        weave(rec(best, "A"), rec(places3), "bbbbbbabbbabbbabbbba")
        moves(t)
        if t + 1 < RO:
            ghosts(t + 1)
            perm("B")
            perm("A")
            weave(rec(step, "B"), rec(step, "A"), "ab" * 5)
            weave(rec(requests, t), rec(prep_b, t + 1), "aabababaabaaaaaa")

    for k, (a, b) in enumerate(part):
        ts(("DB", a, b), ("XT", a, b), 0.0, OP.is_lt)
        mm((ban[k], 0, 448), ("IDB", 0, 128), ("XT", a, b), True, False)
        mm((ban[k], 0, 448), ("EMN", 0, 128), ("DB", a, b), False, True)
        if k % 2:
            cp(("YO", a, b), (ban[k], 0, 448))
        else:
            act(("YO", a, b), (ban[k], 0, 448))
        dma("Y", "st%d" % k, T.y[:, a:b], T["YO"][:, a:b], [("YO", a, b)], [])
    for s in sorted(total):
        if clock["G"].get(s, 0) < total[s]:
            g.wait_ge(T.sem[s], total[s])
